import numpy as np
import ml_dtypes


def mxq(x, axis, fmt="e4m3"):
    dtype, down = {"e4m3": (ml_dtypes.float8_e4m3fn, 7), "e5m2": (ml_dtypes.float8_e5m2, 14)}[fmt]
    v = np.moveaxis(np.asarray(x, np.float32).astype(ml_dtypes.bfloat16).astype(np.float64), axis, -1)
    blocks = v.reshape(v.shape[:-1] + (-1, 32))
    amax = np.abs(blocks).max(-1, keepdims=True)
    byte = np.maximum(np.where(amax > 0, np.frexp(amax)[1] - 1 + 127, 0) - down, 1)
    scale = np.exp2(byte - 127.0)
    codes = (blocks / scale).astype(np.float32).astype(dtype).astype(np.float64)
    return np.moveaxis((codes * scale).reshape(v.shape), -1, axis)


WIDE = False


def mx_kscale(k):
    if not WIDE:
        return np.ones(k)
    levels = np.array([10, -10, 5, -5, 0])
    if k % 512:
        return np.exp2(np.random.permutation(np.resize(levels, k // 32))).repeat(32)
    a = np.empty((k // 512, 16))
    for p in range(k // 512):
        a[p, :8] = np.random.permutation(np.resize(levels, 8))
        for g in range(8):
            far = levels[np.abs(levels - a[p, g]) >= 10]
            a[p, g + 8] = far[np.random.randint(len(far))]
    return np.exp2(a.ravel()).repeat(32)


def f64(x):
    return np.asarray(x).astype(np.float64)


def striped(idx):
    return np.tile(idx.reshape(-1, 16).T, (8, 1)).astype(np.uint16)


def unstriped(offs):
    return offs[:16].T.reshape(-1).astype(np.int64)


def gelu(v):
    return 0.5 * v * (1.0 + np.tanh(np.sqrt(2.0 / np.pi) * (v + 0.044715 * v**3)))


K, T, E, C, H, N = 512, 512, 4, 128, 512, 128


def by_expert(wq, xq):
    return np.concatenate([wq[e].T @ xq[:, e * C:(e + 1) * C] for e in range(E)], axis=1)


def setup_inputs():
    n = np.random.standard_normal
    s = mx_kscale(K)[:, None]
    u = mx_kscale(H)
    return {
        "xT": (n((K, T)) * s).astype(np.float32),
        "w1": (n((E + 1, K, H)) / np.sqrt(K) / s[None]).astype(np.float32),
        "w3": (n((E + 1, K, H)) / np.sqrt(K) / s[None] * u[None, None, :]).astype(np.float32),
        "w2": (n((E + 1, H, N)) / np.sqrt(H) / u[None, :, None]).astype(np.float32),
        "gate": np.tile(np.random.uniform(0.2, 1.0, E * C), (N, 1)).astype(np.float32),
        "offs": striped(np.random.permutation(T)[:E * C]),
    }


def reference(xT, w1, w3, w2, gate, offs):
    idx = unstriped(offs)
    w1q, w3q, w2q = mxq(f64(w1), 1, "e4m3"), mxq(f64(w3), 1, "e4m3"), mxq(f64(w2), 1, "e4m3")
    xs = mxq(f64(xT), 0, "e4m3")
    hs = gelu(w1q[E].T @ xs) * (w3q[E].T @ xs)
    ys = w2q[E].T @ mxq(hs, 0, "e4m3")
    xq = mxq(f64(xT)[:, idx], 0, "e4m3")
    h = gelu(by_expert(w1q, xq))
    h = h * by_expert(w3q, xq)
    y = by_expert(w2q, mxq(h, 0, "e4m3"))
    out = ys
    out[:, idx] += f64(gate) * y
    return out

@@ -1,0 +1,338 @@
+from contextlib import ExitStack
+
+import concourse.mybir as mybir
+
+K, T, E, C, H, N = 512, 512, 4, 128, 512, 128
+FLOPS = 2 * (2 * T) * (2 * K * H + H * N)
+
+F32 = mybir.dt.float32
+BF16 = mybir.dt.bfloat16
+U32 = mybir.dt.uint32
+U16 = mybir.dt.uint16
+U8 = mybir.dt.uint8
+FP8X4 = mybir.dt.float8_e4m3fn_x4
+GELU = mybir.ActivationFunctionType.Gelu_apprx_tanh
+MULT = mybir.AluOpType.mult
+ADD = mybir.AluOpType.add
+
+P = 128
+PACK = 4
+SHARED = E
+HALF = T // 2
+
+
+def tile_moe_shr_glu_gelu_kernel(tc, xT, w1, w3, w2, gate, offs, out):
+    nc = tc.nc
+    with ExitStack() as ctx:
+        keep = ctx.enter_context(tc.tile_pool(name="keep", bufs=1))
+        work = ctx.enter_context(tc.tile_pool(name="work", bufs=4))
+        psum = ctx.enter_context(tc.psum_pool(name="psum", bufs=1))
+
+        offsets = keep.tile([P, T // 16], U16, name="offsets")
+        x_raw = [keep.tile([P, 2, T], F32, name=f"x_raw{u}") for u in range(2)]
+        x_rows = xT.rearrange("(p u h) t -> p u h t", u=2, h=2)
+        nc.sync.dma_start(x_raw[0][:], x_rows[:, 0])
+        nc.sync.dma_start(offsets[:], offs)
+        nc.sync.dma_start(x_raw[1][:], x_rows[:, 1])
+
+        w_raw = {}
+
+        def load(name, src, e):
+            raw = keep.tile([P, PACK, src.shape[2]], F32, name=f"{name}_raw{e}", tag=f"{name}_raw{e}", align_bytes=64)
+            nc.sync.dma_start(raw[:], src[e].rearrange("(p j) c -> p j c", j=PACK))
+            w_raw[name, e] = raw
+
+        w2_raw = {}
+
+        def load_w2(key, lo, hi):
+            w2_raw[key] = keep.tile([P, hi - lo, PACK * N], F32, name=f"w2_raw{key}")
+            nc.sync.dma_start(w2_raw[key][:], w2[lo:hi].rearrange("e (p j) n -> p e (j n)", j=PACK))
+
+        gates = keep.tile([P, T], F32, name="gates")
+        load("w1", w1, SHARED)
+        load("w3", w3, SHARED)
+        load_w2(2, SHARED, SHARED + 1)
+        load("w1", w1, 0)
+        load("w3", w3, 0)
+        load_w2(0, 0, 2)
+        load("w1", w1, 1)
+        load("w3", w3, 1)
+        load("w1", w1, 2)
+        load("w3", w3, 2)
+        nc.sync.dma_start(gates[:], gate)
+        load("w1", w1, 3)
+        load("w3", w3, 3)
+        load_w2(1, 2, 4)
+
+        tiny = keep.tile([P, 2], F32, name="tiny")
+        nc.gpsimd.memset(tiny[:], 0.0)
+        nc.scalar.activation(tiny[:, 1:2], tiny[:, 0:1], GELU)
+
+        x_pairs = [keep.tile([P, T, 2], BF16, name=f"x_pairs{u}", align_bytes=64) for u in range(2)]
+        x_slots = keep.tile([P, T, PACK], BF16, name="x_slots", align_bytes=64)
+        x_words = x_slots[:].rearrange("p s j -> p (s j)").bitcast(U32).rearrange("p (s u) -> p s u", u=2)
+        x_codes = keep.tile([P, T], U32, name="x_codes", align_bytes=64)
+        x_scales = keep.tile([P, T], U8, name="x_scales", align_bytes=64)
+        XS = 0
+        x_view = [r[:].rearrange("p h t -> p t h") for r in x_raw]
+        nc.vector.tensor_copy(x_pairs[0][:, XS:], x_view[0][:, XS:])
+        if XS:
+            nc.scalar.copy(x_pairs[0][:, :XS], x_view[0][:, :XS])
+        nc.scalar.copy(x_pairs[1][:], x_view[1])
+        for u in range(2):
+            window = x_pairs[u][:].rearrange("p t h -> p (t h)").bitcast(U32)
+            for s in range(2):
+                nc.vector.tensor_copy(
+                    x_words[:, s * HALF : (s + 1) * HALF, u],
+                    window.indirect(offsets[:, s * HALF // 16 : (s + 1) * HALF // 16]),
+                )
+        nc.vector.quantize_mx(
+            out=x_codes[:].bitcast(FP8X4), scales=x_scales[:], in_=x_slots[:].rearrange("p s j -> p (s j)")
+        )
+
+        codes = {}
+        scales = {}
+        grouped = {}
+        S1 = {SHARED: 104, 0: 48, 1: 88, 2: 88, 3: 96}
+        S3 = {SHARED: 96, 0: 56, 1: 80, 2: 96, 3: 56}
+
+        def new_weight(name, e, width):
+            grouped[name, e] = keep.tile([P, width * PACK], BF16, name=f"{name}_grouped{e}", align_bytes=64)
+            codes[name, e] = keep.tile([P, width], U32, name=f"{name}_codes{e}", align_bytes=64)
+            scales[name, e] = keep.tile([P, width], U8, name=f"{name}_scales{e}", align_bytes=64)
+
+        def cast_hidden(engine, name, e, lo, hi):
+            if lo == hi:
+                return
+            dst = grouped[name, e][:].rearrange("p (t m j) -> p m j t", t=PACK, j=PACK)
+            src = w_raw[name, e][:].rearrange("p j (m t) -> p m j t", t=PACK)
+            engine(dst[:, lo:hi], src[:, lo:hi])
+
+        def prepare(name, e):
+            new_weight(name, e, H)
+            split = (S1 if name == "w1" else S3)[e]
+            cast_hidden(nc.scalar.copy, name, e, 0, split)
+            cast_hidden(nc.vector.tensor_copy, name, e, split, P)
+
+        def prepare_out(engine, key):
+            width = w2_raw[key].shape[1] * N
+            new_weight("w2", key, width)
+            engine(
+                grouped["w2", key][:].rearrange("p (e n j) -> p e n j", n=N, j=PACK),
+                w2_raw[key][:].rearrange("p e (j n) -> p e n j", j=PACK),
+            )
+
+        def quantize_weight(name, e):
+            nc.vector.quantize_mx(
+                out=codes[name, e][:].bitcast(FP8X4), scales=scales[name, e][:], in_=grouped[name, e][:]
+            )
+
+        gelu_in = {}
+        gelus = {}
+        linear = {}
+        gated = {}
+        h_codes = {}
+        h_scales = {}
+
+        def hidden_product(acc, name, e, g):
+            for t in range(PACK):
+                cols = slice(t * P, (t + 1) * P)
+                slots = slice(g * C, (g + 1) * C)
+                nc.tensor.matmul_mx(
+                    out=acc[:, t, :],
+                    lhsT=codes[name, e][:, cols].bitcast(FP8X4),
+                    lhsT_scale=scales[name, e][:, cols],
+                    rhs=x_codes[:, slots].bitcast(FP8X4),
+                    rhs_scale=x_scales[:, slots],
+                    start=True,
+                    stop=True,
+                )
+
+        def mm_gelu(e, g):
+            gelu_in[e, g] = psum.tile([P, PACK, C], F32, name="gelu_acc", bufs=3)
+            hidden_product(gelu_in[e, g], "w1", e, g)
+
+        def new_gelu(*units, tag):
+            tile = keep.tile([P, len(units) * C, PACK], F32, name=f"gelu_{tag}", tag=tag, align_bytes=64)
+            for i, unit in enumerate(units):
+                gelus[unit] = tile[:, i * C : (i + 1) * C]
+
+        def apply_gelu(e, g):
+            nc.scalar.activation(gelus[e, g], gelu_in[e, g][:].rearrange("p t s -> p s t"), GELU)
+
+        def mm_linear(e, g):
+            linear[e, g] = psum.tile([P, PACK, C], F32, name="linear_acc", bufs=2)
+            hidden_product(linear[e, g], "w3", e, g)
+
+        def new_hidden(e, lo, hi, tag=None):
+            label = f"{e}_{lo}"
+            tag = tag or f"gated{label}"
+            gated[e, lo] = keep.tile([P, hi - lo, PACK], BF16, name=f"gated{label}", tag=tag, align_bytes=64)
+            h_codes[e, lo] = keep.tile([P, hi - lo], U32, name=f"h_codes{label}", align_bytes=64)
+            h_scales[e, lo] = keep.tile([P, hi - lo], U8, name=f"h_scales{label}", align_bytes=64)
+
+        def gate_hidden(e, base, lo, hi):
+            g = lo // C
+            here = slice(lo - g * C, hi - g * C)
+            nc.vector.tensor_tensor(
+                gated[e, base][:, lo - base : hi - base],
+                gelus[e, g][:, here],
+                linear[e, g][:, :, here].rearrange("p t s -> p s t"),
+                MULT,
+            )
+
+        def quantize_hidden(e, base):
+            nc.vector.quantize_mx(
+                out=h_codes[e, base][:].bitcast(FP8X4),
+                scales=h_scales[e, base][:],
+                in_=gated[e, base][:].rearrange("p s t -> p (s t)"),
+            )
+
+        def second_layer(acc, e, base, lo, hi):
+            key, i = (2, 0) if e == SHARED else divmod(e, 2)
+            cols = slice(i * N, (i + 1) * N)
+            slots = slice(lo - base, hi - base)
+            nc.tensor.matmul_mx(
+                out=acc,
+                lhsT=codes["w2", key][:, cols].bitcast(FP8X4),
+                lhsT_scale=scales["w2", key][:, cols],
+                rhs=h_codes[e, base][:, slots].bitcast(FP8X4),
+                rhs_scale=h_scales[e, base][:, slots],
+                start=True,
+                stop=True,
+            )
+
+        shared_acc = psum.tile([P, T], F32, name="shared_acc")
+        result = keep.tile([P, T], F32, name="result")
+        routed_acc = {}
+        weighted = {}
+        total = {}
+
+        def shared_out(g, base):
+            lo = g * C
+            second_layer(shared_acc[:, lo : lo + C], SHARED, base, lo, lo + C)
+
+        def new_routed(lo, hi):
+            routed_acc[lo] = psum.tile([P, hi - lo], F32, name="routed_acc", bufs=2)
+
+        def route(base, e, lo, hi):
+            second_layer(routed_acc[base][:, lo - base : hi - base], e, lo, lo, hi)
+
+        def weigh(base, lo, hi):
+            weighted[lo] = work.tile([P, hi - lo], F32, name="weighted")
+            nc.vector.tensor_tensor(
+                weighted[lo][:], routed_acc[base][:, lo - base : hi - base], gates[:, lo:hi], MULT
+            )
+
+        def add_shared(lo, hi):
+            total[lo] = work.tile([P, hi - lo], F32, name="total")
+            nc.vector.tensor_tensor(total[lo][:], weighted[lo][:], shared_acc[:, lo:hi], ADD)
+
+        def scatter(lo, hi):
+            nc.vector.tensor_copy(result[:].indirect(offsets[:, lo // 16 : hi // 16]), total[lo][:])
+
+        new_gelu(*[(SHARED, g) for g in range(E)], tag="gelu_shared")
+        prepare("w1", SHARED)
+        quantize_weight("w1", SHARED)
+        mm_gelu(SHARED, 0)
+        prepare("w3", SHARED)
+        mm_gelu(SHARED, 1)
+        apply_gelu(SHARED, 0)
+        prepare_out(nc.scalar.copy, 2)
+        quantize_weight("w3", SHARED)
+        quantize_weight("w2", 2)
+        mm_linear(SHARED, 0)
+        mm_gelu(SHARED, 2)
+        mm_linear(SHARED, 1)
+        apply_gelu(SHARED, 1)
+        new_hidden(SHARED, 0, HALF)
+        new_hidden(SHARED, HALF, T)
+        gate_hidden(SHARED, 0, 0, C)
+        mm_linear(SHARED, 2)
+        apply_gelu(SHARED, 2)
+        mm_gelu(SHARED, 3)
+        prepare("w1", 0)
+        gate_hidden(SHARED, 0, C, 2 * C)
+        apply_gelu(SHARED, 3)
+        mm_linear(SHARED, 3)
+        quantize_hidden(SHARED, 0)
+        gate_hidden(SHARED, HALF, 2 * C, 3 * C)
+        quantize_weight("w1", 0)
+        mm_gelu(0, 0)
+        prepare("w3", 0)
+        gate_hidden(SHARED, HALF, 3 * C, 4 * C)
+        quantize_hidden(SHARED, HALF)
+        shared_out(0, 0)
+        shared_out(1, 0)
+        quantize_weight("w3", 0)
+        mm_linear(0, 0)
+        shared_out(2, HALF)
+        shared_out(3, HALF)
+        prepare_out(nc.scalar.copy, 0)
+        prepare("w1", 1)
+        quantize_weight("w1", 1)
+        mm_gelu(1, 1)
+        prepare("w3", 1)
+        quantize_weight("w3", 1)
+        mm_linear(1, 1)
+        quantize_weight("w2", 0)
+        new_gelu((0, 0), (1, 1), tag="w3_raw1")
+        apply_gelu(0, 0)
+        apply_gelu(1, 1)
+        for e in (0, 1):
+            new_hidden(e, e * C, (e + 1) * C)
+            gate_hidden(e, e * C, e * C, (e + 1) * C)
+        for e in (0, 1):
+            quantize_hidden(e, e * C)
+        for e in (0, 1):
+            lo, hi = e * C, (e + 1) * C
+            new_routed(lo, hi)
+            route(lo, e, lo, hi)
+        for e in (0, 1):
+            weigh(e * C, e * C, (e + 1) * C)
+        for e in (0, 1):
+            add_shared(e * C, (e + 1) * C)
+        prepare("w1", 2)
+        quantize_weight("w1", 2)
+        mm_gelu(2, 2)
+        for e in (0, 1):
+            scatter(e * C, (e + 1) * C)
+        prepare("w3", 2)
+        quantize_weight("w3", 2)
+        mm_linear(2, 2)
+        prepare("w1", 3)
+        quantize_weight("w1", 3)
+        mm_gelu(3, 3)
+        prepare("w3", 3)
+        quantize_weight("w3", 3)
+        mm_linear(3, 3)
+        new_gelu((2, 2), (3, 3), tag="gelu_back")
+        apply_gelu(2, 2)
+        apply_gelu(3, 3)
+        prepare_out(nc.scalar.copy, 1)
+        quantize_weight("w2", 1)
+        new_hidden(2, 2 * C, 3 * C, tag="w3_raw3")
+        gate_hidden(2, 2 * C, 2 * C, 3 * C)
+        STEP = C // 1
+        ends = [(lo, lo + STEP) for lo in range(3 * C, 4 * C, STEP)]
+        for lo, hi in ends:
+            new_hidden(3, lo, hi)
+            gate_hidden(3, lo, lo, hi)
+        quantize_hidden(2, 2 * C)
+        for lo, hi in ends:
+            quantize_hidden(3, lo)
+        new_routed(2 * C, 3 * C)
+        new_routed(3 * C, 4 * C)
+        route(2 * C, 2, 2 * C, 3 * C)
+        for lo, hi in ends:
+            route(3 * C, 3, lo, hi)
+        weigh(2 * C, 2 * C, 3 * C)
+        add_shared(2 * C, 3 * C)
+        for lo, hi in ends:
+            weigh(3 * C, lo, hi)
+        scatter(2 * C, 3 * C)
+        for lo, hi in ends:
+            add_shared(lo, hi)
+        for lo, hi in ends:
+            scatter(lo, hi)
+        nc.sync.dma_start(out, result[:])

@@ -20,12 +20,18 @@ PACK = 4
 SHARED = E
 HALF = T // 2
 
+V_FIRST = 32
+V_W1 = 48
+V_W3 = 64
+V_LAST = 84
+MARGIN = C * PACK // 2
+LAP = 16
+
 
 def tile_moe_shr_glu_gelu_kernel(tc, xT, w1, w3, w2, gate, offs, out):
     nc = tc.nc
     with ExitStack() as ctx:
         keep = ctx.enter_context(tc.tile_pool(name="keep", bufs=1))
-        work = ctx.enter_context(tc.tile_pool(name="work", bufs=4))
         psum = ctx.enter_context(tc.psum_pool(name="psum", bufs=1))
 
         offsets = keep.tile([P, T // 16], U16, name="offsets")
@@ -35,34 +41,50 @@ def tile_moe_shr_glu_gelu_kernel(tc, xT, w1, w3, w2, gate, offs, out):
         nc.sync.dma_start(offsets[:], offs)
         nc.sync.dma_start(x_raw[1][:], x_rows[:, 1])
 
-        w_raw = {}
+        raw = {}
 
         def load(name, src, e):
-            raw = keep.tile([P, PACK, src.shape[2]], F32, name=f"{name}_raw{e}", tag=f"{name}_raw{e}", align_bytes=64)
-            nc.sync.dma_start(raw[:], src[e].rearrange("(p j) c -> p j c", j=PACK))
-            w_raw[name, e] = raw
+            tile = keep.tile([P, PACK, H], F32, name=f"{name}_raw{e}", tag=f"{name}_raw{e}", align_bytes=64)
+            raw[name, e] = tile[:]
+            nc.sync.dma_start(tile[:], src[e].rearrange("(p j) c -> p j c", j=PACK))
 
-        w2_raw = {}
+        wide = {}
 
-        def load_w2(key, lo, hi):
-            w2_raw[key] = keep.tile([P, hi - lo, PACK * N], F32, name=f"w2_raw{key}")
-            nc.sync.dma_start(w2_raw[key][:], w2[lo:hi].rearrange("e (p j) n -> p e (j n)", j=PACK))
+        def load_wide(e):
+            wide[e] = keep.tile([P, PACK * H + 2 * MARGIN], F32, name=f"w1_wide{e}", align_bytes=64)
+            flat = wide[e][:, MARGIN : MARGIN + PACK * H]
+            raw["w1", e] = flat.rearrange("p (j c) -> p j c", j=PACK)
+            nc.sync.dma_start(flat, w1[e].rearrange("(p j) c -> p (j c)", j=PACK))
 
-        gates = keep.tile([P, T], F32, name="gates")
+        def load_w2(lo, hi):
+            raw["w2", lo] = keep.tile([P, hi - lo, PACK * N], F32, name=f"w2_raw{lo}")
+            nc.sync.dma_start(raw["w2", lo][:], w2[lo:hi].rearrange("e (p j) n -> p e (j n)", j=PACK))
+
+        gates = {}
+
+        def load_gate(lo, hi):
+            tile = keep.tile([P, (hi - lo) * C], F32, name=f"gates{lo}")
+            nc.sync.dma_start(tile[:], gate[:, lo * C : hi * C])
+            for e in range(lo, hi):
+                gates[e] = tile[:, (e - lo) * C : (e - lo + 1) * C]
+
         load("w1", w1, SHARED)
         load("w3", w3, SHARED)
-        load_w2(2, SHARED, SHARED + 1)
-        load("w1", w1, 0)
-        load("w3", w3, 0)
-        load_w2(0, 0, 2)
-        load("w1", w1, 1)
-        load("w3", w3, 1)
-        load("w1", w1, 2)
-        load("w3", w3, 2)
-        nc.sync.dma_start(gates[:], gate)
-        load("w1", w1, 3)
+        load_wide(3)
         load("w3", w3, 3)
-        load_w2(1, 2, 4)
+        load_wide(2)
+        load_w2(3, 5)
+        load("w3", w3, 2)
+        load_gate(3, 4)
+        load_wide(1)
+        load_w2(2, 3)
+        load("w3", w3, 1)
+        load_gate(2, 3)
+        load_wide(0)
+        load_w2(1, 2)
+        load("w3", w3, 0)
+        load_gate(0, 2)
+        load_w2(0, 1)
 
         tiny = keep.tile([P, 2], F32, name="tiny")
         nc.gpsimd.memset(tiny[:], 0.0)
@@ -73,12 +95,8 @@ def tile_moe_shr_glu_gelu_kernel(tc, xT, w1, w3, w2, gate, offs, out):
         x_words = x_slots[:].rearrange("p s j -> p (s j)").bitcast(U32).rearrange("p (s u) -> p s u", u=2)
         x_codes = keep.tile([P, T], U32, name="x_codes", align_bytes=64)
         x_scales = keep.tile([P, T], U8, name="x_scales", align_bytes=64)
-        XS = 0
-        x_view = [r[:].rearrange("p h t -> p t h") for r in x_raw]
-        nc.vector.tensor_copy(x_pairs[0][:, XS:], x_view[0][:, XS:])
-        if XS:
-            nc.scalar.copy(x_pairs[0][:, :XS], x_view[0][:, :XS])
-        nc.scalar.copy(x_pairs[1][:], x_view[1])
+        nc.vector.tensor_copy(x_pairs[0][:], x_raw[0][:].rearrange("p h t -> p t h"))
+        nc.scalar.copy(x_pairs[1][:], x_raw[1][:].rearrange("p h t -> p t h"))
         for u in range(2):
             window = x_pairs[u][:].rearrange("p t h -> p (t h)").bitcast(U32)
             for s in range(2):
@@ -86,58 +104,47 @@ def tile_moe_shr_glu_gelu_kernel(tc, xT, w1, w3, w2, gate, offs, out):
                     x_words[:, s * HALF : (s + 1) * HALF, u],
                     window.indirect(offsets[:, s * HALF // 16 : (s + 1) * HALF // 16]),
                 )
-        nc.vector.quantize_mx(
-            out=x_codes[:].bitcast(FP8X4), scales=x_scales[:], in_=x_slots[:].rearrange("p s j -> p (s j)")
-        )
 
         codes = {}
         scales = {}
         grouped = {}
-        S1 = {SHARED: 104, 0: 48, 1: 88, 2: 88, 3: 96}
-        S3 = {SHARED: 96, 0: 56, 1: 80, 2: 96, 3: 56}
 
-        def new_weight(name, e, width):
-            grouped[name, e] = keep.tile([P, width * PACK], BF16, name=f"{name}_grouped{e}", align_bytes=64)
-            codes[name, e] = keep.tile([P, width], U32, name=f"{name}_codes{e}", align_bytes=64)
-            scales[name, e] = keep.tile([P, width], U8, name=f"{name}_scales{e}", align_bytes=64)
+        def new_operand(key, width, source=None):
+            label = "_".join(str(part) for part in key)
+            if source is None:
+                source = keep.tile([P, width * PACK], BF16, name=f"grouped_{label}", align_bytes=64)[:]
+            grouped[key] = source
+            codes[key] = keep.tile([P, width], U32, name=f"codes_{label}", align_bytes=64)
+            scales[key] = keep.tile([P, width], U8, name=f"scales_{label}", align_bytes=64)
 
-        def cast_hidden(engine, name, e, lo, hi):
-            if lo == hi:
-                return
-            dst = grouped[name, e][:].rearrange("p (t m j) -> p m j t", t=PACK, j=PACK)
-            src = w_raw[name, e][:].rearrange("p j (m t) -> p m j t", t=PACK)
-            engine(dst[:, lo:hi], src[:, lo:hi])
+        def quantize(key):
+            nc.vector.quantize_mx(out=codes[key][:].bitcast(FP8X4), scales=scales[key][:], in_=grouped[key])
 
-        def prepare(name, e):
-            new_weight(name, e, H)
-            split = (S1 if name == "w1" else S3)[e]
-            cast_hidden(nc.scalar.copy, name, e, 0, split)
-            cast_hidden(nc.vector.tensor_copy, name, e, split, P)
+        def cast_first(name, e, front, back=0):
+            new_operand((name, e), H)
+            dst = grouped[name, e].rearrange("p (t m j) -> p m j t", t=PACK, j=PACK)
+            src = raw[name, e].rearrange("p j (m t) -> p m j t", t=PACK)
+            nc.vector.tensor_copy(dst[:, :front], src[:, :front])
+            if back:
+                nc.vector.tensor_copy(dst[:, P - back :], src[:, P - back :])
+            nc.scalar.copy(dst[:, front : P - back], src[:, front : P - back])
 
-        def prepare_out(engine, key):
-            width = w2_raw[key].shape[1] * N
-            new_weight("w2", key, width)
-            engine(
-                grouped["w2", key][:].rearrange("p (e n j) -> p e n j", n=N, j=PACK),
-                w2_raw[key][:].rearrange("p e (j n) -> p e n j", j=PACK),
+        def cast_second(lo):
+            new_operand(("w2", lo), raw["w2", lo].shape[1] * N)
+            nc.scalar.copy(
+                grouped["w2", lo].rearrange("p (e n j) -> p e n j", n=N, j=PACK),
+                raw["w2", lo][:].rearrange("p e (j n) -> p e n j", j=PACK),
             )
 
-        def quantize_weight(name, e):
-            nc.vector.quantize_mx(
-                out=codes[name, e][:].bitcast(FP8X4), scales=scales[name, e][:], in_=grouped[name, e][:]
-            )
-
-        gelu_in = {}
+        sums = {}
         gelus = {}
-        linear = {}
-        gated = {}
-        h_codes = {}
-        h_scales = {}
 
-        def hidden_product(acc, name, e, g):
+        def first_layer(name, e, g):
+            acc = psum.tile([P, PACK, C], F32, name=f"{name}_acc", bufs=3 if name == "w1" else 2)
+            sums[name, e, g] = acc
+            slots = slice(g * C, (g + 1) * C)
             for t in range(PACK):
                 cols = slice(t * P, (t + 1) * P)
-                slots = slice(g * C, (g + 1) * C)
                 nc.tensor.matmul_mx(
                     out=acc[:, t, :],
                     lhsT=codes[name, e][:, cols].bitcast(FP8X4),
@@ -148,191 +155,115 @@ def tile_moe_shr_glu_gelu_kernel(tc, xT, w1, w3, w2, gate, offs, out):
                     stop=True,
                 )
 
-        def mm_gelu(e, g):
-            gelu_in[e, g] = psum.tile([P, PACK, C], F32, name="gelu_acc", bufs=3)
-            hidden_product(gelu_in[e, g], "w1", e, g)
+        shared_out = {}
 
-        def new_gelu(*units, tag):
-            tile = keep.tile([P, len(units) * C, PACK], F32, name=f"gelu_{tag}", tag=tag, align_bytes=64)
+        def new_gelu(units, groups, tag):
+            width = len(units) * C * PACK
+            tile = keep.tile([P, width + len(groups) * C], F32, name=f"gelu_{tag}", tag=tag, align_bytes=64)
             for i, unit in enumerate(units):
-                gelus[unit] = tile[:, i * C : (i + 1) * C]
+                gelus[unit] = tile[:, i * C * PACK : (i + 1) * C * PACK].rearrange("p (s t) -> p s t", t=PACK)
+            for i, g in enumerate(groups):
+                shared_out[g] = tile[:, width + i * C : width + (i + 1) * C]
+            return tile[:, width:] if groups else None
 
-        def apply_gelu(e, g):
-            nc.scalar.activation(gelus[e, g], gelu_in[e, g][:].rearrange("p t s -> p s t"), GELU)
+        def gelu(e, g):
+            nc.scalar.activation(gelus[e, g], sums["w1", e, g][:].rearrange("p t s -> p s t"), GELU)
 
-        def mm_linear(e, g):
-            linear[e, g] = psum.tile([P, PACK, C], F32, name="linear_acc", bufs=2)
-            hidden_product(linear[e, g], "w3", e, g)
-
-        def new_hidden(e, lo, hi, tag=None):
-            label = f"{e}_{lo}"
-            tag = tag or f"gated{label}"
-            gated[e, lo] = keep.tile([P, hi - lo, PACK], BF16, name=f"gated{label}", tag=tag, align_bytes=64)
-            h_codes[e, lo] = keep.tile([P, hi - lo], U32, name=f"h_codes{label}", align_bytes=64)
-            h_scales[e, lo] = keep.tile([P, hi - lo], U8, name=f"h_scales{label}", align_bytes=64)
-
-        def gate_hidden(e, base, lo, hi):
-            g = lo // C
-            here = slice(lo - g * C, hi - g * C)
+        def product(e, g, source=None):
+            new_operand(("h", e, g), C, source)
             nc.vector.tensor_tensor(
-                gated[e, base][:, lo - base : hi - base],
-                gelus[e, g][:, here],
-                linear[e, g][:, :, here].rearrange("p t s -> p s t"),
+                grouped["h", e, g].rearrange("p (s t) -> p s t", t=PACK),
+                gelus[e, g],
+                sums["w3", e, g][:].rearrange("p t s -> p s t"),
                 MULT,
             )
 
-        def quantize_hidden(e, base):
-            nc.vector.quantize_mx(
-                out=h_codes[e, base][:].bitcast(FP8X4),
-                scales=h_scales[e, base][:],
-                in_=gated[e, base][:].rearrange("p s t -> p (s t)"),
-            )
-
-        def second_layer(acc, e, base, lo, hi):
-            key, i = (2, 0) if e == SHARED else divmod(e, 2)
-            cols = slice(i * N, (i + 1) * N)
-            slots = slice(lo - base, hi - base)
+        def second_layer(acc, e, g):
+            lo = min(e, 3)
+            cols = slice((e - lo) * N, (e - lo + 1) * N)
             nc.tensor.matmul_mx(
                 out=acc,
-                lhsT=codes["w2", key][:, cols].bitcast(FP8X4),
-                lhsT_scale=scales["w2", key][:, cols],
-                rhs=h_codes[e, base][:, slots].bitcast(FP8X4),
-                rhs_scale=h_scales[e, base][:, slots],
+                lhsT=codes["w2", lo][:, cols].bitcast(FP8X4),
+                lhsT_scale=scales["w2", lo][:, cols],
+                rhs=codes["h", e, g][:].bitcast(FP8X4),
+                rhs_scale=scales["h", e, g][:],
                 start=True,
                 stop=True,
             )
 
-        shared_acc = psum.tile([P, T], F32, name="shared_acc")
         result = keep.tile([P, T], F32, name="result")
-        routed_acc = {}
         weighted = {}
-        total = {}
 
-        def shared_out(g, base):
-            lo = g * C
-            second_layer(shared_acc[:, lo : lo + C], SHARED, base, lo, lo + C)
+        def shared_second(lo, hi, dst):
+            acc = psum.tile([P, (hi - lo) * C], F32, name="shared_acc")
+            for g in range(lo, hi):
+                second_layer(acc[:, (g - lo) * C : (g - lo + 1) * C], SHARED, g)
+            nc.scalar.copy(dst, acc[:])
 
-        def new_routed(lo, hi):
-            routed_acc[lo] = psum.tile([P, hi - lo], F32, name="routed_acc", bufs=2)
+        def routed_second(e):
+            acc = psum.tile([P, C], F32, name="routed_acc", bufs=2)
+            second_layer(acc[:], e, e)
+            weighted[e] = keep.tile([P, C], F32, name=f"weighted{e}")
+            nc.vector.tensor_tensor(weighted[e][:], acc[:], gates[e], MULT)
 
-        def route(base, e, lo, hi):
-            second_layer(routed_acc[base][:, lo - base : hi - base], e, lo, lo, hi)
-
-        def weigh(base, lo, hi):
-            weighted[lo] = work.tile([P, hi - lo], F32, name="weighted")
+        def scatter(e):
             nc.vector.tensor_tensor(
-                weighted[lo][:], routed_acc[base][:, lo - base : hi - base], gates[:, lo:hi], MULT
+                result[:].indirect(offsets[:, e * C // 16 : (e + 1) * C // 16]),
+                weighted[e][:],
+                shared_out[e],
+                ADD,
             )
 
-        def add_shared(lo, hi):
-            total[lo] = work.tile([P, hi - lo], F32, name="total")
-            nc.vector.tensor_tensor(total[lo][:], weighted[lo][:], shared_acc[:, lo:hi], ADD)
+        cast_first("w1", SHARED, V_FIRST)
+        nc.vector.quantize_mx(
+            out=x_codes[:].bitcast(FP8X4), scales=x_scales[:], in_=x_slots[:].rearrange("p s j -> p (s j)")
+        )
+        quantize(("w1", SHARED))
+        cast_first("w3", SHARED, V_LAST)
+        waiting = [(SHARED, 3), (SHARED, 2)]
+        new_gelu(waiting, [], f"w3_raw{SHARED}")
+        for unit in waiting:
+            first_layer("w1", *unit)
+        quantize(("w3", SHARED))
+        for unit in waiting:
+            first_layer("w3", *unit)
+        for unit in waiting:
+            gelu(*unit)
 
-        def scatter(lo, hi):
-            nc.vector.tensor_copy(result[:].indirect(offsets[:, lo // 16 : hi // 16]), total[lo][:])
-
-        new_gelu(*[(SHARED, g) for g in range(E)], tag="gelu_shared")
-        prepare("w1", SHARED)
-        quantize_weight("w1", SHARED)
-        mm_gelu(SHARED, 0)
-        prepare("w3", SHARED)
-        mm_gelu(SHARED, 1)
-        apply_gelu(SHARED, 0)
-        prepare_out(nc.scalar.copy, 2)
-        quantize_weight("w3", SHARED)
-        quantize_weight("w2", 2)
-        mm_linear(SHARED, 0)
-        mm_gelu(SHARED, 2)
-        mm_linear(SHARED, 1)
-        apply_gelu(SHARED, 1)
-        new_hidden(SHARED, 0, HALF)
-        new_hidden(SHARED, HALF, T)
-        gate_hidden(SHARED, 0, 0, C)
-        mm_linear(SHARED, 2)
-        apply_gelu(SHARED, 2)
-        mm_gelu(SHARED, 3)
-        prepare("w1", 0)
-        gate_hidden(SHARED, 0, C, 2 * C)
-        apply_gelu(SHARED, 3)
-        mm_linear(SHARED, 3)
-        quantize_hidden(SHARED, 0)
-        gate_hidden(SHARED, HALF, 2 * C, 3 * C)
-        quantize_weight("w1", 0)
-        mm_gelu(0, 0)
-        prepare("w3", 0)
-        gate_hidden(SHARED, HALF, 3 * C, 4 * C)
-        quantize_hidden(SHARED, HALF)
-        shared_out(0, 0)
-        shared_out(1, 0)
-        quantize_weight("w3", 0)
-        mm_linear(0, 0)
-        shared_out(2, HALF)
-        shared_out(3, HALF)
-        prepare_out(nc.scalar.copy, 0)
-        prepare("w1", 1)
-        quantize_weight("w1", 1)
-        mm_gelu(1, 1)
-        prepare("w3", 1)
-        quantize_weight("w3", 1)
-        mm_linear(1, 1)
-        quantize_weight("w2", 0)
-        new_gelu((0, 0), (1, 1), tag="w3_raw1")
-        apply_gelu(0, 0)
-        apply_gelu(1, 1)
-        for e in (0, 1):
-            new_hidden(e, e * C, (e + 1) * C)
-            gate_hidden(e, e * C, e * C, (e + 1) * C)
-        for e in (0, 1):
-            quantize_hidden(e, e * C)
-        for e in (0, 1):
-            lo, hi = e * C, (e + 1) * C
-            new_routed(lo, hi)
-            route(lo, e, lo, hi)
-        for e in (0, 1):
-            weigh(e * C, e * C, (e + 1) * C)
-        for e in (0, 1):
-            add_shared(e * C, (e + 1) * C)
-        prepare("w1", 2)
-        quantize_weight("w1", 2)
-        mm_gelu(2, 2)
-        for e in (0, 1):
-            scatter(e * C, (e + 1) * C)
-        prepare("w3", 2)
-        quantize_weight("w3", 2)
-        mm_linear(2, 2)
-        prepare("w1", 3)
-        quantize_weight("w1", 3)
-        mm_gelu(3, 3)
-        prepare("w3", 3)
-        quantize_weight("w3", 3)
-        mm_linear(3, 3)
-        new_gelu((2, 2), (3, 3), tag="gelu_back")
-        apply_gelu(2, 2)
-        apply_gelu(3, 3)
-        prepare_out(nc.scalar.copy, 1)
-        quantize_weight("w2", 1)
-        new_hidden(2, 2 * C, 3 * C, tag="w3_raw3")
-        gate_hidden(2, 2 * C, 2 * C, 3 * C)
-        STEP = C // 1
-        ends = [(lo, lo + STEP) for lo in range(3 * C, 4 * C, STEP)]
-        for lo, hi in ends:
-            new_hidden(3, lo, hi)
-            gate_hidden(3, lo, lo, hi)
-        quantize_hidden(2, 2 * C)
-        for lo, hi in ends:
-            quantize_hidden(3, lo)
-        new_routed(2 * C, 3 * C)
-        new_routed(3 * C, 4 * C)
-        route(2 * C, 2, 2 * C, 3 * C)
-        for lo, hi in ends:
-            route(3 * C, 3, lo, hi)
-        weigh(2 * C, 2 * C, 3 * C)
-        add_shared(2 * C, 3 * C)
-        for lo, hi in ends:
-            weigh(3 * C, lo, hi)
-        scatter(2 * C, 3 * C)
-        for lo, hi in ends:
-            add_shared(lo, hi)
-        for lo, hi in ends:
-            scatter(lo, hi)
+        for e in (3, 2, 1, 0):
+            units = [(SHARED, e - 2), (e, e)] if e >= 2 else [(e, e)]
+            share = V_W1 if e else V_LAST
+            cast_first("w1", e, share // 2, share // 2)
+            for unit, start in zip(waiting, (LAP, MARGIN + PACK * H - LAP)):
+                product(*unit, wide[e][:, start : start + MARGIN].bitcast(BF16))
+            quantize(("w1", e))
+            for unit in waiting:
+                quantize(("h", *unit))
+            if e >= 2:
+                first_layer("w3", SHARED, e - 2)
+            for unit in units:
+                first_layer("w1", *unit)
+            if e < 3:
+                cast_second(e + 1)
+                quantize(("w2", e + 1))
+            cast_first("w3", e, V_W3 if e else V_LAST)
+            if e < 3:
+                routed_second(e + 1)
+            quantize(("w3", e))
+            first_layer("w3", e, e)
+            groups = {2: [1, 2, 3], 1: [0]}.get(e, [])
+            shared_sums = new_gelu(units, groups, f"w3_raw{e}")
+            if groups:
+                shared_second(groups[0], groups[-1] + 1, shared_sums)
+            if e < 3:
+                scatter(e + 1)
+            for unit in units:
+                gelu(*unit)
+            waiting = units
+        product(0, 0)
+        cast_second(0)
+        quantize(("w2", 0))
+        quantize(("h", 0, 0))
+        routed_second(0)
+        scatter(0)
         nc.sync.dma_start(out, result[:])

@@ -21,9 +21,9 @@ SHARED = E
 HALF = T // 2
 
 V_FIRST = 32
-V_W1 = 48
-V_W3 = 64
-V_LAST = 84
+V_HALF = 64
+V_W3 = 56
+V_LAST = 48
 MARGIN = C * PACK // 2
 LAP = 16
 
@@ -43,18 +43,13 @@ def tile_moe_shr_glu_gelu_kernel(tc, xT, w1, w3, w2, gate, offs, out):
 
         raw = {}
 
-        def load(name, src, e):
-            tile = keep.tile([P, PACK, H], F32, name=f"{name}_raw{e}", tag=f"{name}_raw{e}", align_bytes=64)
-            raw[name, e] = tile[:]
-            nc.sync.dma_start(tile[:], src[e].rearrange("(p j) c -> p j c", j=PACK))
-
         wide = {}
 
-        def load_wide(e):
-            wide[e] = keep.tile([P, PACK * H + 2 * MARGIN], F32, name=f"w1_wide{e}", align_bytes=64)
-            flat = wide[e][:, MARGIN : MARGIN + PACK * H]
-            raw["w1", e] = flat.rearrange("p (j c) -> p j c", j=PACK)
-            nc.sync.dma_start(flat, w1[e].rearrange("(p j) c -> p (j c)", j=PACK))
+        def load(name, src, e, before=0, after=0):
+            wide[name, e] = keep.tile([P, before + PACK * H + after], F32, name=f"{name}_raw{e}", align_bytes=64)
+            flat = wide[name, e][:, before : before + PACK * H]
+            raw[name, e] = flat.rearrange("p (j c) -> p j c", j=PACK)
+            nc.sync.dma_start(flat, src[e].rearrange("(p j) c -> p (j c)", j=PACK))
 
         def load_w2(lo, hi):
             raw["w2", lo] = keep.tile([P, hi - lo, PACK * N], F32, name=f"w2_raw{lo}")
@@ -70,19 +65,19 @@ def tile_moe_shr_glu_gelu_kernel(tc, xT, w1, w3, w2, gate, offs, out):
 
         load("w1", w1, SHARED)
         load("w3", w3, SHARED)
-        load_wide(3)
+        load("w1", w1, 3, MARGIN, MARGIN)
         load("w3", w3, 3)
-        load_wide(2)
+        load("w1", w1, 2, MARGIN, MARGIN)
         load_w2(3, 5)
-        load("w3", w3, 2)
+        load("w3", w3, 2, 0, C)
         load_gate(3, 4)
-        load_wide(1)
+        load("w1", w1, 1, MARGIN, MARGIN)
         load_w2(2, 3)
-        load("w3", w3, 1)
+        load("w3", w3, 1, 0, C)
         load_gate(2, 3)
-        load_wide(0)
+        load("w1", w1, 0, MARGIN, MARGIN)
         load_w2(1, 2)
-        load("w3", w3, 0)
+        load("w3", w3, 0, 0, 2 * C)
         load_gate(0, 2)
         load_w2(0, 1)
 
@@ -99,7 +94,7 @@ def tile_moe_shr_glu_gelu_kernel(tc, xT, w1, w3, w2, gate, offs, out):
         nc.scalar.copy(x_pairs[1][:], x_raw[1][:].rearrange("p h t -> p t h"))
         for u in range(2):
             window = x_pairs[u][:].rearrange("p t h -> p (t h)").bitcast(U32)
-            for s in range(2):
+            for s in (1, 0):
                 nc.vector.tensor_copy(
                     x_words[:, s * HALF : (s + 1) * HALF, u],
                     window.indirect(offsets[:, s * HALF // 16 : (s + 1) * HALF // 16]),
@@ -117,8 +112,14 @@ def tile_moe_shr_glu_gelu_kernel(tc, xT, w1, w3, w2, gate, offs, out):
             codes[key] = keep.tile([P, width], U32, name=f"codes_{label}", align_bytes=64)
             scales[key] = keep.tile([P, width], U8, name=f"scales_{label}", align_bytes=64)
 
-        def quantize(key):
-            nc.vector.quantize_mx(out=codes[key][:].bitcast(FP8X4), scales=scales[key][:], in_=grouped[key])
+        def quantize(key, parts=1):
+            step = codes[key].shape[1] // parts
+            for lo in range(0, parts * step, step):
+                nc.vector.quantize_mx(
+                    out=codes[key][:, lo : lo + step].bitcast(FP8X4),
+                    scales=scales[key][:, lo : lo + step],
+                    in_=grouped[key][:, lo * PACK : (lo + step) * PACK],
+                )
 
         def cast_first(name, e, front, back=0):
             new_operand((name, e), H)
@@ -140,7 +141,7 @@ def tile_moe_shr_glu_gelu_kernel(tc, xT, w1, w3, w2, gate, offs, out):
         gelus = {}
 
         def first_layer(name, e, g):
-            acc = psum.tile([P, PACK, C], F32, name=f"{name}_acc", bufs=3 if name == "w1" else 2)
+            acc = psum.tile([P, PACK, C], F32, name=f"{name}_acc", bufs=2)
             sums[name, e, g] = acc
             slots = slice(g * C, (g + 1) * C)
             for t in range(PACK):
@@ -157,24 +158,18 @@ def tile_moe_shr_glu_gelu_kernel(tc, xT, w1, w3, w2, gate, offs, out):
 
         shared_out = {}
 
-        def new_gelu(units, groups, tag):
-            width = len(units) * C * PACK
-            tile = keep.tile([P, width + len(groups) * C], F32, name=f"gelu_{tag}", tag=tag, align_bytes=64)
-            for i, unit in enumerate(units):
-                gelus[unit] = tile[:, i * C * PACK : (i + 1) * C * PACK].rearrange("p (s t) -> p s t", t=PACK)
-            for i, g in enumerate(groups):
-                shared_out[g] = tile[:, width + i * C : width + (i + 1) * C]
-            return tile[:, width:] if groups else None
-
-        def gelu(e, g):
-            nc.scalar.activation(gelus[e, g], sums["w1", e, g][:].rearrange("p t s -> p s t"), GELU)
+        def gelu(e, g, host, on_vector, i):
+            first = on_vector * PACK
+            rows = raw["w3", host][:, 2 * i : 2 * i + 2, first : first + C * PACK // 2]
+            gelus[e, g] = rows.rearrange("p r (s t) -> p r s t", t=PACK)
+            nc.scalar.activation(gelus[e, g], sums["w1", e, g][:].rearrange("p t (r s) -> p r s t", r=2), GELU)
 
         def product(e, g, source=None):
             new_operand(("h", e, g), C, source)
             nc.vector.tensor_tensor(
-                grouped["h", e, g].rearrange("p (s t) -> p s t", t=PACK),
+                grouped["h", e, g].rearrange("p (r s t) -> p r s t", r=2, t=PACK),
                 gelus[e, g],
-                sums["w3", e, g][:].rearrange("p t s -> p s t"),
+                sums["w3", e, g][:].rearrange("p t (r s) -> p r s t", r=2),
                 MULT,
             )
 
@@ -194,11 +189,16 @@ def tile_moe_shr_glu_gelu_kernel(tc, xT, w1, w3, w2, gate, offs, out):
         result = keep.tile([P, T], F32, name="result")
         weighted = {}
 
-        def shared_second(lo, hi, dst):
-            acc = psum.tile([P, (hi - lo) * C], F32, name="shared_acc")
+        shared_acc = psum.tile([P, T], F32, name="shared_acc")
+
+        def shared_second(g):
+            second_layer(shared_acc[:, g * C : (g + 1) * C], SHARED, g)
+
+        def shared_leave(lo, hi, host):
+            first = PACK * H - LAP
+            nc.scalar.copy(wide["w3", host][:, first : first + (hi - lo) * C], shared_acc[:, lo * C : hi * C])
             for g in range(lo, hi):
-                second_layer(acc[:, (g - lo) * C : (g - lo + 1) * C], SHARED, g)
-            nc.scalar.copy(dst, acc[:])
+                shared_out[g] = wide["w3", host][:, first + (g - lo) * C : first + (g - lo + 1) * C]
 
         def routed_second(e):
             acc = psum.tile([P, C], F32, name="routed_acc", bufs=2)
@@ -214,28 +214,30 @@ def tile_moe_shr_glu_gelu_kernel(tc, xT, w1, w3, w2, gate, offs, out):
                 ADD,
             )
 
+        x_flat = x_slots[:].rearrange("p s j -> p (s j)")
+        for lo in (HALF, 0):
+            nc.vector.quantize_mx(
+                out=x_codes[:, lo : lo + HALF].bitcast(FP8X4),
+                scales=x_scales[:, lo : lo + HALF],
+                in_=x_flat[:, lo * PACK : (lo + HALF) * PACK],
+            )
         cast_first("w1", SHARED, V_FIRST)
-        nc.vector.quantize_mx(
-            out=x_codes[:].bitcast(FP8X4), scales=x_scales[:], in_=x_slots[:].rearrange("p s j -> p (s j)")
-        )
         quantize(("w1", SHARED))
-        cast_first("w3", SHARED, V_LAST)
+        cast_first("w3", SHARED, V_HALF)
         waiting = [(SHARED, 3), (SHARED, 2)]
-        new_gelu(waiting, [], f"w3_raw{SHARED}")
         for unit in waiting:
             first_layer("w1", *unit)
-        quantize(("w3", SHARED))
+        quantize(("w3", SHARED), 2)
         for unit in waiting:
             first_layer("w3", *unit)
-        for unit in waiting:
-            gelu(*unit)
+        for i, unit in enumerate(waiting):
+            gelu(*unit, SHARED, V_HALF, i)
 
         for e in (3, 2, 1, 0):
             units = [(SHARED, e - 2), (e, e)] if e >= 2 else [(e, e)]
-            share = V_W1 if e else V_LAST
-            cast_first("w1", e, share // 2, share // 2)
+            cast_first("w1", e, V_HALF // 2, V_HALF // 2)
             for unit, start in zip(waiting, (LAP, MARGIN + PACK * H - LAP)):
-                product(*unit, wide[e][:, start : start + MARGIN].bitcast(BF16))
+                product(*unit, wide["w1", e][:, start : start + MARGIN].bitcast(BF16))
             quantize(("w1", e))
             for unit in waiting:
                 quantize(("h", *unit))
@@ -246,19 +248,23 @@ def tile_moe_shr_glu_gelu_kernel(tc, xT, w1, w3, w2, gate, offs, out):
             if e < 3:
                 cast_second(e + 1)
                 quantize(("w2", e + 1))
-            cast_first("w3", e, V_W3 if e else V_LAST)
+            share = V_W3 if e else V_LAST
+            cast_first("w3", e, share)
             if e < 3:
                 routed_second(e + 1)
-            quantize(("w3", e))
+            quantize(("w3", e), 2)
             first_layer("w3", e, e)
-            groups = {2: [1, 2, 3], 1: [0]}.get(e, [])
-            shared_sums = new_gelu(units, groups, f"w3_raw{e}")
-            if groups:
-                shared_second(groups[0], groups[-1] + 1, shared_sums)
+            if e == 2:
+                for g in (3, 2, 1):
+                    shared_second(g)
+            if e < 3:
+                shared_leave(e + 1 if e else 0, e + 2, e)
+            if e == 1:
+                shared_second(0)
             if e < 3:
                 scatter(e + 1)
-            for unit in units:
-                gelu(*unit)
+            for i, unit in enumerate(units):
+                gelu(*unit, e, share, i)
             waiting = units
         product(0, 0)
         cast_second(0)

@@ -1,6 +1,7 @@
 from contextlib import ExitStack
 
 import concourse.mybir as mybir
+from concourse.masks import make_identity
 
 K, T, E, C, H, N = 512, 512, 4, 128, 512, 128
 FLOPS = 2 * (2 * T) * (2 * K * H + H * N)
@@ -23,7 +24,7 @@ HALF = T // 2
 V_FIRST = 32
 V_HALF = 64
 V_W3 = 56
-V_LAST = 48
+V_LAST = 84
 MARGIN = C * PACK // 2
 LAP = 16
 
@@ -35,10 +36,13 @@ def tile_moe_shr_glu_gelu_kernel(tc, xT, w1, w3, w2, gate, offs, out):
         psum = ctx.enter_context(tc.psum_pool(name="psum", bufs=1))
 
         offsets = keep.tile([P, T // 16], U16, name="offsets")
-        x_raw = [keep.tile([P, 2, T], F32, name=f"x_raw{u}") for u in range(2)]
+        x_raw = [keep.tile([P, 2, T], F32, name=f"x_raw{u}", tag=f"x_raw{u}") for u in range(2)]
         x_rows = xT.rearrange("(p u h) t -> p u h t", u=2, h=2)
         nc.sync.dma_start(x_raw[0][:], x_rows[:, 0])
         nc.sync.dma_start(offsets[:], offs)
+        gate_rows = keep.tile([P, C], F32, name="gate_rows")
+        nc.gpsimd.memset(gate_rows[:], 0.0)
+        nc.sync.dma_start(gate_rows[:E], gate[0].rearrange("(e s) -> e s", e=E))
         nc.sync.dma_start(x_raw[1][:], x_rows[:, 1])
 
         raw = {}
@@ -55,13 +59,8 @@ def tile_moe_shr_glu_gelu_kernel(tc, xT, w1, w3, w2, gate, offs, out):
             raw["w2", lo] = keep.tile([P, hi - lo, PACK * N], F32, name=f"w2_raw{lo}")
             nc.sync.dma_start(raw["w2", lo][:], w2[lo:hi].rearrange("e (p j) n -> p e (j n)", j=PACK))
 
-        gates = {}
-
-        def load_gate(lo, hi):
-            tile = keep.tile([P, (hi - lo) * C], F32, name=f"gates{lo}")
-            nc.sync.dma_start(tile[:], gate[:, lo * C : hi * C])
-            for e in range(lo, hi):
-                gates[e] = tile[:, (e - lo) * C : (e - lo + 1) * C]
+        identity = keep.tile([P, P], F32, name="identity")
+        make_identity(nc, identity[:])
 
         load("w1", w1, SHARED)
         load("w3", w3, SHARED)
@@ -70,15 +69,12 @@ def tile_moe_shr_glu_gelu_kernel(tc, xT, w1, w3, w2, gate, offs, out):
         load("w1", w1, 2, MARGIN, MARGIN)
         load_w2(3, 5)
         load("w3", w3, 2, 0, C)
-        load_gate(3, 4)
         load("w1", w1, 1, MARGIN, MARGIN)
         load_w2(2, 3)
         load("w3", w3, 1, 0, C)
-        load_gate(2, 3)
         load("w1", w1, 0, MARGIN, MARGIN)
         load_w2(1, 2)
         load("w3", w3, 0, 0, 2 * C)
-        load_gate(0, 2)
         load_w2(0, 1)
 
         tiny = keep.tile([P, 2], F32, name="tiny")
@@ -99,6 +95,18 @@ def tile_moe_shr_glu_gelu_kernel(tc, xT, w1, w3, w2, gate, offs, out):
                     x_words[:, s * HALF : (s + 1) * HALF, u],
                     window.indirect(offsets[:, s * HALF // 16 : (s + 1) * HALF // 16]),
                 )
+
+        turned = psum.tile([P, P], F32, name="gate_acc")
+        nc.tensor.transpose(turned[:], gate_rows[:], identity[:])
+        gate_columns = keep.tile([P, E], F32, name="gate_columns")
+        nc.scalar.copy(gate_columns[:], turned[:, :E])
+        spread = psum.tile([P, T], F32, name="gate_acc")
+        for e in range(E):
+            nc.tensor.transpose(
+                spread[:, e * C : (e + 1) * C], gate_columns[:, e : e + 1].to_broadcast([P, P]), identity[:]
+            )
+        gates = keep.tile([P, T], F32, name="gates", tag="x_raw1")
+        nc.scalar.copy(gates[:], spread[:])
 
         codes = {}
         scales = {}
@@ -121,11 +129,13 @@ def tile_moe_shr_glu_gelu_kernel(tc, xT, w1, w3, w2, gate, offs, out):
                     in_=grouped[key][:, lo * PACK : (lo + step) * PACK],
                 )
 
-        def cast_first(name, e, front, back=0):
+        def cast_first(name, e, front, back=0, cut=0):
             new_operand((name, e), H)
             dst = grouped[name, e].rearrange("p (t m j) -> p m j t", t=PACK, j=PACK)
             src = raw[name, e].rearrange("p j (m t) -> p m j t", t=PACK)
-            nc.vector.tensor_copy(dst[:, :front], src[:, :front])
+            if cut:
+                nc.vector.tensor_copy(dst[:, :cut], src[:, :cut])
+            nc.vector.tensor_copy(dst[:, cut:front], src[:, cut:front])
             if back:
                 nc.vector.tensor_copy(dst[:, P - back :], src[:, P - back :])
             nc.scalar.copy(dst[:, front : P - back], src[:, front : P - back])
@@ -160,16 +170,18 @@ def tile_moe_shr_glu_gelu_kernel(tc, xT, w1, w3, w2, gate, offs, out):
 
         def gelu(e, g, host, on_vector, i):
             first = on_vector * PACK
-            rows = raw["w3", host][:, 2 * i : 2 * i + 2, first : first + C * PACK // 2]
+            count = 2 if host else PACK
+            rows = raw["w3", host][:, count * i : count * (i + 1), first : first + C * PACK // count]
             gelus[e, g] = rows.rearrange("p r (s t) -> p r s t", t=PACK)
-            nc.scalar.activation(gelus[e, g], sums["w1", e, g][:].rearrange("p t (r s) -> p r s t", r=2), GELU)
+            nc.scalar.activation(gelus[e, g], sums["w1", e, g][:].rearrange("p t (r s) -> p r s t", r=count), GELU)
 
         def product(e, g, source=None):
             new_operand(("h", e, g), C, source)
+            count = gelus[e, g].shape[1]
             nc.vector.tensor_tensor(
-                grouped["h", e, g].rearrange("p (r s t) -> p r s t", r=2, t=PACK),
+                grouped["h", e, g].rearrange("p (r s t) -> p r s t", r=count, t=PACK),
                 gelus[e, g],
-                sums["w3", e, g][:].rearrange("p t (r s) -> p r s t", r=2),
+                sums["w3", e, g][:].rearrange("p t (r s) -> p r s t", r=count),
                 MULT,
             )
 
@@ -200,16 +212,19 @@ def tile_moe_shr_glu_gelu_kernel(tc, xT, w1, w3, w2, gate, offs, out):
             for g in range(lo, hi):
                 shared_out[g] = wide["w3", host][:, first + (g - lo) * C : first + (g - lo + 1) * C]
 
-        def routed_second(e):
+        def routed_second(e, host=None):
             acc = psum.tile([P, C], F32, name="routed_acc", bufs=2)
             second_layer(acc[:], e, e)
-            weighted[e] = keep.tile([P, C], F32, name=f"weighted{e}")
-            nc.vector.tensor_tensor(weighted[e][:], acc[:], gates[e], MULT)
+            if host is None:
+                weighted[e] = keep.tile([P, C], F32, name=f"weighted{e}")[:]
+            else:
+                weighted[e] = wide["w3", host][:, :C]
+            nc.vector.tensor_tensor(weighted[e], acc[:], gates[:, e * C : (e + 1) * C], MULT)
 
         def scatter(e):
             nc.vector.tensor_tensor(
                 result[:].indirect(offsets[:, e * C // 16 : (e + 1) * C // 16]),
-                weighted[e][:],
+                weighted[e],
                 shared_out[e],
                 ADD,
             )
@@ -249,9 +264,9 @@ def tile_moe_shr_glu_gelu_kernel(tc, xT, w1, w3, w2, gate, offs, out):
                 cast_second(e + 1)
                 quantize(("w2", e + 1))
             share = V_W3 if e else V_LAST
-            cast_first("w3", e, share)
+            cast_first("w3", e, share, 0, C // PACK if e < 3 else 0)
             if e < 3:
-                routed_second(e + 1)
+                routed_second(e + 1, e)
             quantize(("w3", e), 2)
             first_layer("w3", e, e)
             if e == 2:

@@ -24,7 +24,8 @@ HALF = T // 2
 V_FIRST = 32
 V_HALF = 64
 V_W3 = 56
-V_LAST = 84
+V_W1 = 48
+V_LAST = 80
 MARGIN = C * PACK // 2
 LAP = 16
 
@@ -41,7 +42,7 @@ def tile_moe_shr_glu_gelu_kernel(tc, xT, w1, w3, w2, gate, offs, out):
         nc.sync.dma_start(x_raw[0][:], x_rows[:, 0])
         nc.sync.dma_start(offsets[:], offs)
         gate_rows = keep.tile([P, C], F32, name="gate_rows")
-        nc.gpsimd.memset(gate_rows[:], 0.0)
+        nc.vector.memset(gate_rows[:], 0.0)
         nc.sync.dma_start(gate_rows[:E], gate[0].rearrange("(e s) -> e s", e=E))
         nc.sync.dma_start(x_raw[1][:], x_rows[:, 1])
 
@@ -56,7 +57,7 @@ def tile_moe_shr_glu_gelu_kernel(tc, xT, w1, w3, w2, gate, offs, out):
             nc.sync.dma_start(flat, src[e].rearrange("(p j) c -> p (j c)", j=PACK))
 
         def load_w2(lo, hi):
-            raw["w2", lo] = keep.tile([P, hi - lo, PACK * N], F32, name=f"w2_raw{lo}")
+            raw["w2", lo] = keep.tile([P, hi - lo, PACK * N], F32, name=f"w2_raw{lo}", tag=f"w2_raw{lo}")
             nc.sync.dma_start(raw["w2", lo][:], w2[lo:hi].rearrange("e (p j) n -> p e (j n)", j=PACK))
 
         identity = keep.tile([P, P], F32, name="identity")
@@ -73,9 +74,12 @@ def tile_moe_shr_glu_gelu_kernel(tc, xT, w1, w3, w2, gate, offs, out):
         load_w2(2, 3)
         load("w3", w3, 1, 0, C)
         load("w1", w1, 0, MARGIN, MARGIN)
-        load_w2(1, 2)
-        load("w3", w3, 0, 0, 2 * C)
-        load_w2(0, 1)
+        load("w3", w3, 0)
+        ahead = C * PACK - LAP
+        w2_one = keep.tile([P, ahead + PACK * N], F32, name="w2_one")
+        w2_zero = keep.tile([P, PACK * N], F32, name="w2_zero", align_bytes=64)
+        nc.sync.dma_start(w2_one[:, ahead:], w2[1].rearrange("(p j) n -> p (j n)", j=PACK))
+        nc.sync.dma_start(w2_zero[:], w2[0].rearrange("(p j) n -> p (j n)", j=PACK))
 
         tiny = keep.tile([P, 2], F32, name="tiny")
         nc.gpsimd.memset(tiny[:], 0.0)
@@ -140,6 +144,14 @@ def tile_moe_shr_glu_gelu_kernel(tc, xT, w1, w3, w2, gate, offs, out):
                 nc.vector.tensor_copy(dst[:, P - back :], src[:, P - back :])
             nc.scalar.copy(dst[:, front : P - back], src[:, front : P - back])
 
+        def cast_last(name, e, on_vector):
+            new_operand((name, e), H)
+            dst = grouped[name, e].rearrange("p (t m j) -> p m j t", t=PACK, j=PACK)
+            src = raw[name, e].rearrange("p j (m t) -> p m j t", t=PACK)
+            for t in (0, 2):
+                nc.vector.tensor_copy(dst[:, :on_vector, :, t : t + 2], src[:, :on_vector, :, t : t + 2])
+                nc.scalar.copy(dst[:, on_vector:, :, t : t + 2], src[:, on_vector:, :, t : t + 2])
+
         def cast_second(lo):
             new_operand(("w2", lo), raw["w2", lo].shape[1] * N)
             nc.scalar.copy(
@@ -168,12 +180,14 @@ def tile_moe_shr_glu_gelu_kernel(tc, xT, w1, w3, w2, gate, offs, out):
 
         shared_out = {}
 
-        def gelu(e, g, host, on_vector, i):
+        def rows_of(host, on_vector, i, count):
             first = on_vector * PACK
-            count = 2 if host else PACK
-            rows = raw["w3", host][:, count * i : count * (i + 1), first : first + C * PACK // count]
+            return raw["w3", host][:, count * i : count * (i + 1), first : first + C * PACK // count]
+
+        def gelu(e, g, rows):
             gelus[e, g] = rows.rearrange("p r (s t) -> p r s t", t=PACK)
-            nc.scalar.activation(gelus[e, g], sums["w1", e, g][:].rearrange("p t (r s) -> p r s t", r=count), GELU)
+            source = sums["w1", e, g][:].rearrange("p t (r s) -> p r s t", r=rows.shape[1])
+            nc.scalar.activation(gelus[e, g], source, GELU)
 
         def product(e, g, source=None):
             new_operand(("h", e, g), C, source)
@@ -186,7 +200,7 @@ def tile_moe_shr_glu_gelu_kernel(tc, xT, w1, w3, w2, gate, offs, out):
             )
 
         def second_layer(acc, e, g):
-            lo = min(e, 3)
+            lo = {0: 0, 1: 0, 2: 2, 3: 3, SHARED: 3}[e]
             cols = slice((e - lo) * N, (e - lo + 1) * N)
             nc.tensor.matmul_mx(
                 out=acc,
@@ -246,11 +260,12 @@ def tile_moe_shr_glu_gelu_kernel(tc, xT, w1, w3, w2, gate, offs, out):
         for unit in waiting:
             first_layer("w3", *unit)
         for i, unit in enumerate(waiting):
-            gelu(*unit, SHARED, V_HALF, i)
+            gelu(*unit, rows_of(SHARED, V_HALF, i, 2))
 
         for e in (3, 2, 1, 0):
             units = [(SHARED, e - 2), (e, e)] if e >= 2 else [(e, e)]
-            cast_first("w1", e, V_HALF // 2, V_HALF // 2)
+            end = (V_W1 if e else V_FIRST) // 2
+            cast_first("w1", e, end, end)
             for unit, start in zip(waiting, (LAP, MARGIN + PACK * H - LAP)):
                 product(*unit, wide["w1", e][:, start : start + MARGIN].bitcast(BF16))
             quantize(("w1", e))
@@ -260,11 +275,12 @@ def tile_moe_shr_glu_gelu_kernel(tc, xT, w1, w3, w2, gate, offs, out):
                 first_layer("w3", SHARED, e - 2)
             for unit in units:
                 first_layer("w1", *unit)
+            if e == 0:
+                break
             if e < 3:
                 cast_second(e + 1)
                 quantize(("w2", e + 1))
-            share = V_W3 if e else V_LAST
-            cast_first("w3", e, share, 0, C // PACK if e < 3 else 0)
+            cast_first("w3", e, V_W3, 0, C // PACK if e < 3 else 0)
             if e < 3:
                 routed_second(e + 1, e)
             quantize(("w3", e), 2)
@@ -273,18 +289,33 @@ def tile_moe_shr_glu_gelu_kernel(tc, xT, w1, w3, w2, gate, offs, out):
                 for g in (3, 2, 1):
                     shared_second(g)
             if e < 3:
-                shared_leave(e + 1 if e else 0, e + 2, e)
+                shared_leave(e + 1, e + 2, e)
             if e == 1:
                 shared_second(0)
             if e < 3:
                 scatter(e + 1)
             for i, unit in enumerate(units):
-                gelu(*unit, e, share, i)
+                gelu(*unit, rows_of(e, V_W3, i, 2))
             waiting = units
-        product(0, 0)
-        cast_second(0)
+        first = MARGIN + H + V_FIRST // 2 * PACK
+        nc.scalar.copy(wide["w1", 0][:, first : first + HALF], shared_acc[:, :HALF])
+        for g in range(2):
+            shared_out[g] = wide["w1", 0][:, first + g * C : first + (g + 1) * C]
+        cast_last("w3", 0, V_LAST)
+        quantize(("w3", 0), 2)
+        first_layer("w3", 0, 0)
+        new_operand(("w2", 0), 2 * N)
+        pair = grouped["w2", 0].rearrange("p (e n j) -> p e n j", n=N, j=PACK)
+        one = w2_one[:, ahead:].rearrange("p (j n) -> p n j", j=PACK)
+        for half in (slice(0, N // 2), slice(N // 2, N)):
+            nc.scalar.copy(pair[:, 1, half], one[:, half])
+        nc.vector.tensor_copy(pair[:, 0], w2_zero[:].rearrange("p (j n) -> p n j", j=PACK))
         quantize(("w2", 0))
+        gelu(0, 0, w2_one[:, : C * PACK].rearrange("p (r c) -> p r c", r=1))
+        product(0, 0, w2_zero[:, :MARGIN].bitcast(BF16))
+        routed_second(1)
         quantize(("h", 0, 0))
+        scatter(1)
         routed_second(0)
         scatter(0)
         nc.sync.dma_start(out, result[:])

@@ -23,9 +23,9 @@ HALF = T // 2
 
 V_FIRST = 32
 V_HALF = 64
-V_W3 = 56
-V_W1 = 48
-V_LAST = 80
+V_W3 = 48
+V_TWO = 68
+V_LAST = 72
 MARGIN = C * PACK // 2
 LAP = 16
 
@@ -65,15 +65,15 @@ def tile_moe_shr_glu_gelu_kernel(tc, xT, w1, w3, w2, gate, offs, out):
 
         load("w1", w1, SHARED)
         load("w3", w3, SHARED)
-        load("w1", w1, 3, MARGIN, MARGIN)
+        load("w1", w1, 3, MARGIN)
         load("w3", w3, 3)
-        load("w1", w1, 2, MARGIN, MARGIN)
+        load("w1", w1, 2, MARGIN)
         load_w2(3, 5)
         load("w3", w3, 2, 0, C)
-        load("w1", w1, 1, MARGIN, MARGIN)
+        load("w1", w1, 1, MARGIN)
         load_w2(2, 3)
         load("w3", w3, 1, 0, C)
-        load("w1", w1, 0, MARGIN, MARGIN)
+        load("w1", w1, 0, MARGIN)
         load("w3", w3, 0)
         ahead = C * PACK - LAP
         w2_one = keep.tile([P, ahead + PACK * N], F32, name="w2_one")
@@ -133,16 +133,14 @@ def tile_moe_shr_glu_gelu_kernel(tc, xT, w1, w3, w2, gate, offs, out):
                     in_=grouped[key][:, lo * PACK : (lo + step) * PACK],
                 )
 
-        def cast_first(name, e, front, back=0, cut=0):
+        def cast_first(name, e, front, cut=0):
             new_operand((name, e), H)
             dst = grouped[name, e].rearrange("p (t m j) -> p m j t", t=PACK, j=PACK)
             src = raw[name, e].rearrange("p j (m t) -> p m j t", t=PACK)
             if cut:
                 nc.vector.tensor_copy(dst[:, :cut], src[:, :cut])
             nc.vector.tensor_copy(dst[:, cut:front], src[:, cut:front])
-            if back:
-                nc.vector.tensor_copy(dst[:, P - back :], src[:, P - back :])
-            nc.scalar.copy(dst[:, front : P - back], src[:, front : P - back])
+            nc.scalar.copy(dst[:, front:], src[:, front:])
 
         def cast_last(name, e, on_vector):
             new_operand((name, e), H)
@@ -155,8 +153,8 @@ def tile_moe_shr_glu_gelu_kernel(tc, xT, w1, w3, w2, gate, offs, out):
         def cast_second(lo):
             new_operand(("w2", lo), raw["w2", lo].shape[1] * N)
             nc.scalar.copy(
-                grouped["w2", lo].rearrange("p (e n j) -> p e n j", n=N, j=PACK),
-                raw["w2", lo][:].rearrange("p e (j n) -> p e n j", j=PACK),
+                grouped["w2", lo].rearrange("p (e c i j) -> p e c j i", i=PACK, j=PACK, c=N // PACK),
+                raw["w2", lo][:].rearrange("p e (j c i) -> p e c j i", i=PACK, j=PACK),
             )
 
         sums = {}
@@ -189,11 +187,20 @@ def tile_moe_shr_glu_gelu_kernel(tc, xT, w1, w3, w2, gate, offs, out):
             source = sums["w1", e, g][:].rearrange("p t (r s) -> p r s t", r=rows.shape[1])
             nc.scalar.activation(gelus[e, g], source, GELU)
 
-        def product(e, g, source=None):
-            new_operand(("h", e, g), C, source)
+        hidden = {}
+
+        def new_hidden(units, source):
+            key = ("h", *units[-1])
+            new_operand(key, len(units) * C, source)
+            for i, unit in enumerate(units):
+                hidden[unit] = (key, i)
+            return key
+
+        def product(e, g):
+            key, i = hidden[e, g]
             count = gelus[e, g].shape[1]
             nc.vector.tensor_tensor(
-                grouped["h", e, g].rearrange("p (r s t) -> p r s t", r=count, t=PACK),
+                grouped[key][:, i * C * PACK : (i + 1) * C * PACK].rearrange("p (r s t) -> p r s t", r=count, t=PACK),
                 gelus[e, g],
                 sums["w3", e, g][:].rearrange("p t (r s) -> p r s t", r=count),
                 MULT,
@@ -202,12 +209,13 @@ def tile_moe_shr_glu_gelu_kernel(tc, xT, w1, w3, w2, gate, offs, out):
         def second_layer(acc, e, g):
             lo = {0: 0, 1: 0, 2: 2, 3: 3, SHARED: 3}[e]
             cols = slice((e - lo) * N, (e - lo + 1) * N)
+            key, i = hidden[e, g]
             nc.tensor.matmul_mx(
                 out=acc,
                 lhsT=codes["w2", lo][:, cols].bitcast(FP8X4),
                 lhsT_scale=scales["w2", lo][:, cols],
-                rhs=codes["h", e, g][:].bitcast(FP8X4),
-                rhs_scale=scales["h", e, g][:],
+                rhs=codes[key][:, i * C : (i + 1) * C].bitcast(FP8X4),
+                rhs_scale=scales[key][:, i * C : (i + 1) * C],
                 start=True,
                 stop=True,
             )
@@ -264,13 +272,13 @@ def tile_moe_shr_glu_gelu_kernel(tc, xT, w1, w3, w2, gate, offs, out):
 
         for e in (3, 2, 1, 0):
             units = [(SHARED, e - 2), (e, e)] if e >= 2 else [(e, e)]
-            end = (V_W1 if e else V_FIRST) // 2
-            cast_first("w1", e, end, end)
-            for unit, start in zip(waiting, (LAP, MARGIN + PACK * H - LAP)):
-                product(*unit, wide["w1", e][:, start : start + MARGIN].bitcast(BF16))
-            quantize(("w1", e))
+            share = V_TWO if len(waiting) == 2 else V_FIRST
+            cast_first("w1", e, share, share // 4 * 2)
+            key = new_hidden(waiting, wide["w1", e][:, LAP : LAP + len(waiting) * MARGIN].bitcast(BF16))
             for unit in waiting:
-                quantize(("h", *unit))
+                product(*unit)
+            quantize(("w1", e))
+            quantize(key)
             if e >= 2:
                 first_layer("w3", SHARED, e - 2)
             for unit in units:
@@ -280,10 +288,10 @@ def tile_moe_shr_glu_gelu_kernel(tc, xT, w1, w3, w2, gate, offs, out):
             if e < 3:
                 cast_second(e + 1)
                 quantize(("w2", e + 1))
-            cast_first("w3", e, V_W3, 0, C // PACK if e < 3 else 0)
+            cast_first("w3", e, V_W3, C // PACK if e < 3 else 0)
             if e < 3:
                 routed_second(e + 1, e)
-            quantize(("w3", e), 2)
+            quantize(("w3", e), 2 if e == 3 else 1)
             first_layer("w3", e, e)
             if e == 2:
                 for g in (3, 2, 1):
@@ -297,7 +305,7 @@ def tile_moe_shr_glu_gelu_kernel(tc, xT, w1, w3, w2, gate, offs, out):
             for i, unit in enumerate(units):
                 gelu(*unit, rows_of(e, V_W3, i, 2))
             waiting = units
-        first = MARGIN + H + V_FIRST // 2 * PACK
+        first = MARGIN + H + V_FIRST * PACK
         nc.scalar.copy(wide["w1", 0][:, first : first + HALF], shared_acc[:, :HALF])
         for g in range(2):
             shared_out[g] = wide["w1", 0][:, first + g * C : first + (g + 1) * C]
@@ -305,14 +313,15 @@ def tile_moe_shr_glu_gelu_kernel(tc, xT, w1, w3, w2, gate, offs, out):
         quantize(("w3", 0), 2)
         first_layer("w3", 0, 0)
         new_operand(("w2", 0), 2 * N)
-        pair = grouped["w2", 0].rearrange("p (e n j) -> p e n j", n=N, j=PACK)
-        one = w2_one[:, ahead:].rearrange("p (j n) -> p n j", j=PACK)
-        for half in (slice(0, N // 2), slice(N // 2, N)):
+        pair = grouped["w2", 0].rearrange("p (e c i j) -> p e c j i", i=PACK, j=PACK, e=2)
+        one = w2_one[:, ahead:].rearrange("p (j c i) -> p c j i", i=PACK, j=PACK)
+        for half in (slice(0, N // 8), slice(N // 8, N // 4)):
             nc.scalar.copy(pair[:, 1, half], one[:, half])
-        nc.vector.tensor_copy(pair[:, 0], w2_zero[:].rearrange("p (j n) -> p n j", j=PACK))
+        nc.vector.tensor_copy(pair[:, 0], w2_zero[:].rearrange("p (j c i) -> p c j i", i=PACK, j=PACK))
         quantize(("w2", 0))
         gelu(0, 0, w2_one[:, : C * PACK].rearrange("p (r c) -> p r c", r=1))
-        product(0, 0, w2_zero[:, :MARGIN].bitcast(BF16))
+        new_hidden([(0, 0)], w2_zero[:, :MARGIN].bitcast(BF16))
+        product(0, 0)
         routed_second(1)
         quantize(("h", 0, 0))
         scatter(1)

@@ -135,8 +135,8 @@ def tile_moe_shr_glu_gelu_kernel(tc, xT, w1, w3, w2, gate, offs, out):
 
         def cast_first(name, e, front, cut=0):
             new_operand((name, e), H)
-            dst = grouped[name, e].rearrange("p (t m j) -> p m j t", t=PACK, j=PACK)
-            src = raw[name, e].rearrange("p j (m t) -> p m j t", t=PACK)
+            dst = grouped[name, e].rearrange("p (t m a b) -> p m a t b", t=PACK, a=2, b=2)
+            src = raw[name, e].rearrange("p (a b) (m t) -> p m a t b", b=2, t=PACK)
             if cut:
                 nc.vector.tensor_copy(dst[:, :cut], src[:, :cut])
             nc.vector.tensor_copy(dst[:, cut:front], src[:, cut:front])
@@ -144,18 +144,18 @@ def tile_moe_shr_glu_gelu_kernel(tc, xT, w1, w3, w2, gate, offs, out):
 
         def cast_last(name, e, on_vector):
             new_operand((name, e), H)
-            dst = grouped[name, e].rearrange("p (t m j) -> p m j t", t=PACK, j=PACK)
-            src = raw[name, e].rearrange("p j (m t) -> p m j t", t=PACK)
+            dst = grouped[name, e].rearrange("p (t m a b) -> p m a t b", t=PACK, a=2, b=2)
+            src = raw[name, e].rearrange("p (a b) (m t) -> p m a t b", b=2, t=PACK)
             for t in (0, 2):
                 nc.vector.tensor_copy(dst[:, :on_vector, :, t : t + 2], src[:, :on_vector, :, t : t + 2])
                 nc.scalar.copy(dst[:, on_vector:, :, t : t + 2], src[:, on_vector:, :, t : t + 2])
 
         def cast_second(lo):
             new_operand(("w2", lo), raw["w2", lo].shape[1] * N)
-            nc.scalar.copy(
-                grouped["w2", lo].rearrange("p (e c i j) -> p e c j i", i=PACK, j=PACK, c=N // PACK),
-                raw["w2", lo][:].rearrange("p e (j c i) -> p e c j i", i=PACK, j=PACK),
-            )
+            dst = grouped["w2", lo].rearrange("p (e c i a b) -> p e c a i b", i=PACK, a=2, b=2, c=N // PACK)
+            src = raw["w2", lo][:].rearrange("p e (a b c i) -> p e c a i b", i=PACK, a=2, b=2)
+            for e in range(dst.shape[1]):
+                nc.scalar.copy(dst[:, e], src[:, e])
 
         sums = {}
         gelus = {}
@@ -313,11 +313,11 @@ def tile_moe_shr_glu_gelu_kernel(tc, xT, w1, w3, w2, gate, offs, out):
         quantize(("w3", 0), 2)
         first_layer("w3", 0, 0)
         new_operand(("w2", 0), 2 * N)
-        pair = grouped["w2", 0].rearrange("p (e c i j) -> p e c j i", i=PACK, j=PACK, e=2)
-        one = w2_one[:, ahead:].rearrange("p (j c i) -> p c j i", i=PACK, j=PACK)
+        pair = grouped["w2", 0].rearrange("p (e c i a b) -> p e c a i b", i=PACK, a=2, b=2, e=2)
+        one = w2_one[:, ahead:].rearrange("p (a b c i) -> p c a i b", i=PACK, a=2, b=2)
         for half in (slice(0, N // 8), slice(N // 8, N // 4)):
             nc.scalar.copy(pair[:, 1, half], one[:, half])
-        nc.vector.tensor_copy(pair[:, 0], w2_zero[:].rearrange("p (j c i) -> p c j i", i=PACK, j=PACK))
+        nc.vector.tensor_copy(pair[:, 0], w2_zero[:].rearrange("p (a b c i) -> p c a i b", i=PACK, a=2, b=2))
         quantize(("w2", 0))
         gelu(0, 0, w2_one[:, : C * PACK].rearrange("p (r c) -> p r c", r=1))
         new_hidden([(0, 0)], w2_zero[:, :MARGIN].bitcast(BF16))

@@ -24,6 +24,8 @@ HALF = T // 2
 V_FIRST = 32
 V_HALF = 64
 V_W3 = 48
+V_ONE = 56
+V_WIDE = 72
 V_TWO = 68
 V_LAST = 72
 MARGIN = C * PACK // 2
@@ -100,18 +102,17 @@ def tile_moe_shr_glu_gelu_kernel(tc, xT, w1, w3, w2, gate, offs, out):
                     window.indirect(offsets[:, s * HALF // 16 : (s + 1) * HALF // 16]),
                 )
 
-        turned = psum.tile([P, P], F32, name="gate_acc")
+        turned = psum.tile([P, P], F32, name="routed_acc", bufs=2)
         nc.tensor.transpose(turned[:], gate_rows[:], identity[:])
         gate_columns = keep.tile([P, E], F32, name="gate_columns")
         nc.scalar.copy(gate_columns[:], turned[:, :E])
-        spread = psum.tile([P, T], F32, name="gate_acc")
+        spread = psum.tile([P, T], F32, name="routed_acc", bufs=2)
         for e in range(E):
             nc.tensor.transpose(
                 spread[:, e * C : (e + 1) * C], gate_columns[:, e : e + 1].to_broadcast([P, P]), identity[:]
             )
-        gates = keep.tile([P, T], F32, name="gates", tag="x_raw1")
-        nc.scalar.copy(gates[:], spread[:])
 
+        gates = raw["w1", 3][:, :, V_TWO * PACK : V_TWO * PACK + C]
         codes = {}
         scales = {}
         grouped = {}
@@ -161,7 +162,7 @@ def tile_moe_shr_glu_gelu_kernel(tc, xT, w1, w3, w2, gate, offs, out):
         gelus = {}
 
         def first_layer(name, e, g):
-            acc = psum.tile([P, PACK, C], F32, name=f"{name}_acc", bufs=2)
+            acc = psum.tile([P, PACK, C], F32, name=f"{name}_acc", bufs=2 if name == "w1" else 3)
             sums[name, e, g] = acc
             slots = slice(g * C, (g + 1) * C)
             for t in range(PACK):
@@ -241,7 +242,7 @@ def tile_moe_shr_glu_gelu_kernel(tc, xT, w1, w3, w2, gate, offs, out):
                 weighted[e] = keep.tile([P, C], F32, name=f"weighted{e}")[:]
             else:
                 weighted[e] = wide["w3", host][:, :C]
-            nc.vector.tensor_tensor(weighted[e], acc[:], gates[:, e * C : (e + 1) * C], MULT)
+            nc.vector.tensor_tensor(weighted[e], acc[:], gates[:, e], MULT)
 
         def scatter(e):
             nc.vector.tensor_tensor(
@@ -261,26 +262,35 @@ def tile_moe_shr_glu_gelu_kernel(tc, xT, w1, w3, w2, gate, offs, out):
         cast_first("w1", SHARED, V_FIRST)
         quantize(("w1", SHARED))
         cast_first("w3", SHARED, V_HALF)
-        waiting = [(SHARED, 3), (SHARED, 2)]
-        for unit in waiting:
+        waiting = [(SHARED, 3), (SHARED, 2), (SHARED, 1)]
+        for unit in waiting[:2]:
             first_layer("w1", *unit)
         quantize(("w3", SHARED), 2)
         for unit in waiting:
             first_layer("w3", *unit)
-        for i, unit in enumerate(waiting):
+        for i, unit in enumerate(waiting[:2]):
             gelu(*unit, rows_of(SHARED, V_HALF, i, 2))
+        first_layer("w1", *waiting[2])
+        third = keep.tile([P, 1, C * PACK], F32, name="third")
+        gelu(*waiting[2], third[:])
 
         for e in (3, 2, 1, 0):
-            units = [(SHARED, e - 2), (e, e)] if e >= 2 else [(e, e)]
-            share = V_TWO if len(waiting) == 2 else V_FIRST
+            units = [(SHARED, 0), (e, e)] if e == 3 else [(e, e)]
+            share = V_TWO if len(waiting) >= 2 else V_ONE
             cast_first("w1", e, share, share // 4 * 2)
-            key = new_hidden(waiting, wide["w1", e][:, LAP : LAP + len(waiting) * MARGIN].bitcast(BF16))
+            if e == 3:
+                nc.scalar.copy(gates, spread[:].rearrange("p (e s) -> p e s", e=E))
+            pair = waiting[:2]
+            keys = [new_hidden(pair, wide["w1", e][:, LAP : LAP + len(pair) * MARGIN].bitcast(BF16))]
+            if len(waiting) == 3:
+                keys.append(new_hidden(waiting[2:], raw["w1", e][:, 1, :MARGIN].bitcast(BF16)))
             for unit in waiting:
                 product(*unit)
             quantize(("w1", e))
-            quantize(key)
-            if e >= 2:
-                first_layer("w3", SHARED, e - 2)
+            for key in keys:
+                quantize(key)
+            if e == 3:
+                first_layer("w3", SHARED, 0)
             for unit in units:
                 first_layer("w1", *unit)
             if e == 0:
@@ -288,24 +298,22 @@ def tile_moe_shr_glu_gelu_kernel(tc, xT, w1, w3, w2, gate, offs, out):
             if e < 3:
                 cast_second(e + 1)
                 quantize(("w2", e + 1))
-            cast_first("w3", e, V_W3, C // PACK if e < 3 else 0)
+            cast_first("w3", e, V_WIDE if e < 3 else V_W3, C // PACK if e < 3 else 0)
             if e < 3:
                 routed_second(e + 1, e)
             quantize(("w3", e), 2 if e == 3 else 1)
             first_layer("w3", e, e)
             if e == 2:
-                for g in (3, 2, 1):
+                for g in (3, 2, 1, 0):
                     shared_second(g)
             if e < 3:
                 shared_leave(e + 1, e + 2, e)
-            if e == 1:
-                shared_second(0)
             if e < 3:
                 scatter(e + 1)
             for i, unit in enumerate(units):
-                gelu(*unit, rows_of(e, V_W3, i, 2))
+                gelu(*unit, rows_of(e, V_W3, i, 2) if e == 3 else rows_of(e, V_WIDE, i, 4))
             waiting = units
-        first = MARGIN + H + V_FIRST * PACK
+        first = MARGIN + H + V_ONE * PACK
         nc.scalar.copy(wide["w1", 0][:, first : first + HALF], shared_acc[:, :HALF])
         for g in range(2):
             shared_out[g] = wide["w1", 0][:, first + g * C : first + (g + 1) * C]

@@ -179,14 +179,13 @@ def tile_moe_shr_glu_gelu_kernel(tc, xT, w1, w3, w2, gate, offs, out):
 
         shared_out = {}
 
-        def rows_of(host, on_vector, i, count):
-            first = on_vector * PACK
-            return raw["w3", host][:, count * i : count * (i + 1), first : first + C * PACK // count]
+        def rows_of(host, on_vector, i):
+            first = on_vector * PACK + i * C
+            return raw["w3", host][:, :, first : first + C]
 
         def gelu(e, g, rows):
-            gelus[e, g] = rows.rearrange("p r (s t) -> p r s t", t=PACK)
-            source = sums["w1", e, g][:].rearrange("p t (r s) -> p r s t", r=rows.shape[1])
-            nc.scalar.activation(gelus[e, g], source, GELU)
+            gelus[e, g] = rows
+            nc.scalar.activation(rows, sums["w1", e, g][:], GELU)
 
         hidden = {}
 
@@ -199,11 +198,10 @@ def tile_moe_shr_glu_gelu_kernel(tc, xT, w1, w3, w2, gate, offs, out):
 
         def product(e, g):
             key, i = hidden[e, g]
-            count = gelus[e, g].shape[1]
             nc.vector.tensor_tensor(
-                grouped[key][:, i * C * PACK : (i + 1) * C * PACK].rearrange("p (r s t) -> p r s t", r=count, t=PACK),
-                gelus[e, g],
-                sums["w3", e, g][:].rearrange("p t (r s) -> p r s t", r=count),
+                grouped[key][:, i * C * PACK : (i + 1) * C * PACK].rearrange("p (q s t) -> p q t s", s=2, t=PACK),
+                gelus[e, g].rearrange("p t (q s) -> p q t s", s=2),
+                sums["w3", e, g][:].rearrange("p t (q s) -> p q t s", s=2),
                 MULT,
             )
 
@@ -269,9 +267,9 @@ def tile_moe_shr_glu_gelu_kernel(tc, xT, w1, w3, w2, gate, offs, out):
         for unit in waiting:
             first_layer("w3", *unit)
         for i, unit in enumerate(waiting[:2]):
-            gelu(*unit, rows_of(SHARED, V_HALF, i, 2))
+            gelu(*unit, rows_of(SHARED, V_HALF, i))
         first_layer("w1", *waiting[2])
-        third = keep.tile([P, 1, C * PACK], F32, name="third")
+        third = keep.tile([P, PACK, C], F32, name="third")
         gelu(*waiting[2], third[:])
 
         for e in (3, 2, 1, 0):
@@ -311,7 +309,7 @@ def tile_moe_shr_glu_gelu_kernel(tc, xT, w1, w3, w2, gate, offs, out):
             if e < 3:
                 scatter(e + 1)
             for i, unit in enumerate(units):
-                gelu(*unit, rows_of(e, V_W3, i, 2) if e == 3 else rows_of(e, V_WIDE, i, 4))
+                gelu(*unit, rows_of(e, V_WIDE if e < 3 else V_W3, i))
             waiting = units
         first = MARGIN + H + V_ONE * PACK
         nc.scalar.copy(wide["w1", 0][:, first : first + HALF], shared_acc[:, :HALF])
@@ -327,7 +325,7 @@ def tile_moe_shr_glu_gelu_kernel(tc, xT, w1, w3, w2, gate, offs, out):
             nc.scalar.copy(pair[:, 1, half], one[:, half])
         nc.vector.tensor_copy(pair[:, 0], w2_zero[:].rearrange("p (a b c i) -> p c a i b", i=PACK, a=2, b=2))
         quantize(("w2", 0))
-        gelu(0, 0, w2_one[:, : C * PACK].rearrange("p (r c) -> p r c", r=1))
+        gelu(0, 0, w2_one[:, : C * PACK].rearrange("p (t s) -> p t s", t=PACK))
         new_hidden([(0, 0)], w2_zero[:, :MARGIN].bitcast(BF16))
         product(0, 0)
         routed_second(1)

@@ -45,7 +45,7 @@ def tile_moe_shr_glu_gelu_kernel(tc, xT, w1, w3, w2, gate, offs, out):
         nc.sync.dma_start(offsets[:], offs)
         gate_rows = keep.tile([P, C], F32, name="gate_rows")
         nc.vector.memset(gate_rows[:], 0.0)
-        nc.sync.dma_start(gate_rows[:E], gate[0].rearrange("(e s) -> e s", e=E))
+        nc.scalar.dma_start(gate_rows[:E], gate[0].rearrange("(e s) -> e s", e=E))
         nc.sync.dma_start(x_raw[1][:], x_rows[:, 1])
 
         raw = {}

@@ -24,10 +24,10 @@ HALF = T // 2
 V_FIRST = 32
 V_HALF = 64
 V_W3 = 48
-V_ONE = 56
-V_WIDE = 72
+V_ONE = 48
+V_WIDE = 80
 V_TWO = 68
-V_LAST = 72
+V_LAST = 80
 MARGIN = C * PACK // 2
 LAP = 16
 
@@ -36,6 +36,7 @@ def tile_moe_shr_glu_gelu_kernel(tc, xT, w1, w3, w2, gate, offs, out):
     nc = tc.nc
     with ExitStack() as ctx:
         keep = ctx.enter_context(tc.tile_pool(name="keep", bufs=1))
+        tail = ctx.enter_context(tc.tile_pool(name="tail", bufs=1))
         psum = ctx.enter_context(tc.psum_pool(name="psum", bufs=1))
 
         offsets = keep.tile([P, T // 16], U16, name="offsets")
@@ -59,7 +60,7 @@ def tile_moe_shr_glu_gelu_kernel(tc, xT, w1, w3, w2, gate, offs, out):
             nc.sync.dma_start(flat, src[e].rearrange("(p j) c -> p (j c)", j=PACK))
 
         def load_w2(lo, hi):
-            raw["w2", lo] = keep.tile([P, hi - lo, PACK * N], F32, name=f"w2_raw{lo}", tag=f"w2_raw{lo}")
+            raw["w2", lo] = keep.tile([P, hi - lo, PACK * N], F32, name=f"w2_raw{lo}", align_bytes=64)
             nc.sync.dma_start(raw["w2", lo][:], w2[lo:hi].rearrange("e (p j) n -> p e (j n)", j=PACK))
 
         identity = keep.tile([P, P], F32, name="identity")
@@ -76,12 +77,12 @@ def tile_moe_shr_glu_gelu_kernel(tc, xT, w1, w3, w2, gate, offs, out):
         load_w2(2, 3)
         load("w3", w3, 1, 0, C)
         load("w1", w1, 0, MARGIN)
-        load("w3", w3, 0)
-        ahead = C * PACK - LAP
-        w2_one = keep.tile([P, ahead + PACK * N], F32, name="w2_one")
-        w2_zero = keep.tile([P, PACK * N], F32, name="w2_zero", align_bytes=64)
+        load("w3", w3, 0, 0, C * PACK)
+        ahead = MARGIN - LAP
+        w2_one = keep.tile([P, ahead + PACK * N], F32, name="w2_one", align_bytes=64)
         nc.sync.dma_start(w2_one[:, ahead:], w2[1].rearrange("(p j) n -> p (j n)", j=PACK))
-        nc.sync.dma_start(w2_zero[:], w2[0].rearrange("(p j) n -> p (j n)", j=PACK))
+        raw["w2", 0] = tail.tile([P, 1, PACK * N], F32, name="w2_raw0", align_bytes=64, offset=0)
+        nc.sync.dma_start(raw["w2", 0][:], w2[0:1].rearrange("e (p j) n -> p e (j n)", j=PACK))
 
         tiny = keep.tile([P, 2], F32, name="tiny")
         nc.gpsimd.memset(tiny[:], 0.0)
@@ -147,9 +148,11 @@ def tile_moe_shr_glu_gelu_kernel(tc, xT, w1, w3, w2, gate, offs, out):
             new_operand((name, e), H)
             dst = grouped[name, e].rearrange("p (t m a b) -> p m a t b", t=PACK, a=2, b=2)
             src = raw[name, e].rearrange("p (a b) (m t) -> p m a t b", b=2, t=PACK)
+            edge = P - LAP // PACK
+            nc.scalar.copy(dst[:, edge:], src[:, edge:])
             for t in (0, 2):
                 nc.vector.tensor_copy(dst[:, :on_vector, :, t : t + 2], src[:, :on_vector, :, t : t + 2])
-                nc.scalar.copy(dst[:, on_vector:, :, t : t + 2], src[:, on_vector:, :, t : t + 2])
+                nc.scalar.copy(dst[:, on_vector:edge, :, t : t + 2], src[:, on_vector:edge, :, t : t + 2])
 
         def cast_second(lo):
             new_operand(("w2", lo), raw["w2", lo].shape[1] * N)
@@ -206,7 +209,7 @@ def tile_moe_shr_glu_gelu_kernel(tc, xT, w1, w3, w2, gate, offs, out):
             )
 
         def second_layer(acc, e, g):
-            lo = {0: 0, 1: 0, 2: 2, 3: 3, SHARED: 3}[e]
+            lo = min(e, 3)
             cols = slice((e - lo) * N, (e - lo + 1) * N)
             key, i = hidden[e, g]
             nc.tensor.matmul_mx(
@@ -284,9 +287,12 @@ def tile_moe_shr_glu_gelu_kernel(tc, xT, w1, w3, w2, gate, offs, out):
                 keys.append(new_hidden(waiting[2:], raw["w1", e][:, 1, :MARGIN].bitcast(BF16)))
             for unit in waiting:
                 product(*unit)
-            quantize(("w1", e))
+            if len(waiting) > 1:
+                quantize(("w1", e))
             for key in keys:
                 quantize(key)
+            if len(waiting) == 1:
+                quantize(("w1", e))
             if e == 3:
                 first_layer("w3", SHARED, 0)
             for unit in units:
@@ -311,25 +317,33 @@ def tile_moe_shr_glu_gelu_kernel(tc, xT, w1, w3, w2, gate, offs, out):
             for i, unit in enumerate(units):
                 gelu(*unit, rows_of(e, V_WIDE if e < 3 else V_W3, i))
             waiting = units
-        first = MARGIN + H + V_ONE * PACK
-        nc.scalar.copy(wide["w1", 0][:, first : first + HALF], shared_acc[:, :HALF])
-        for g in range(2):
-            shared_out[g] = wide["w1", 0][:, first + g * C : first + (g + 1) * C]
         cast_last("w3", 0, V_LAST)
         quantize(("w3", 0), 2)
         first_layer("w3", 0, 0)
-        new_operand(("w2", 0), 2 * N)
-        pair = grouped["w2", 0].rearrange("p (e c i a b) -> p e c a i b", i=PACK, a=2, b=2, e=2)
-        one = w2_one[:, ahead:].rearrange("p (a b c i) -> p c a i b", i=PACK, a=2, b=2)
-        for half in (slice(0, N // 8), slice(N // 8, N // 4)):
-            nc.scalar.copy(pair[:, 1, half], one[:, half])
-        nc.vector.tensor_copy(pair[:, 0], w2_zero[:].rearrange("p (a b c i) -> p c a i b", i=PACK, a=2, b=2))
-        quantize(("w2", 0))
-        gelu(0, 0, w2_one[:, : C * PACK].rearrange("p (t s) -> p t s", t=PACK))
-        new_hidden([(0, 0)], w2_zero[:, :MARGIN].bitcast(BF16))
+        first = PACK * H - LAP
+        gelu(0, 0, wide["w3", 0][:, first : first + C * PACK].rearrange("p (t s) -> p t s", t=PACK))
+        new_operand(("w2", 1), N, grouped["w3", 0][:, : N * PACK])
+        dst = grouped["w2", 1].rearrange("p (c i a b) -> p c a i b", i=PACK, a=2, b=2)
+        src = w2_one[:, ahead:].rearrange("p (a b c i) -> p c a i b", i=PACK, a=2, b=2)
+        for half in (slice(N // 8, N // 4), slice(0, N // 8)):
+            nc.vector.tensor_copy(dst[:, half], src[:, half])
+        for lo in (N // 2, 0):
+            nc.vector.quantize_mx(
+                out=codes["w2", 1][:, lo : lo + N // 2].bitcast(FP8X4),
+                scales=scales["w2", 1][:, lo : lo + N // 2],
+                in_=grouped["w2", 1][:, lo * PACK : (lo + N // 2) * PACK],
+            )
+        key = new_hidden([(0, 0)], w2_one[:, :MARGIN].bitcast(BF16))
+        codes[key] = tail.tile([P, C], U32, name="last_codes", align_bytes=64, offset=0)
         product(0, 0)
         routed_second(1)
-        quantize(("h", 0, 0))
+        cast_second(0)
+        quantize(("w2", 0))
+        quantize(key)
+        last_shared = tail.tile([P, HALF], F32, name="last_shared", align_bytes=64, offset=C * 4)
+        nc.scalar.copy(last_shared[:], shared_acc[:, :HALF])
+        for g in range(2):
+            shared_out[g] = last_shared[:, g * C : (g + 1) * C]
         scatter(1)
         routed_second(0)
         scatter(0)

@@ -40,7 +40,7 @@ def tile_moe_shr_glu_gelu_kernel(tc, xT, w1, w3, w2, gate, offs, out):
         psum = ctx.enter_context(tc.psum_pool(name="psum", bufs=1))
 
         offsets = keep.tile([P, T // 16], U16, name="offsets")
-        x_raw = [keep.tile([P, 2, T], F32, name=f"x_raw{u}", tag=f"x_raw{u}") for u in range(2)]
+        x_raw = [keep.tile([P, 2, T], F32, name=f"x_raw{u}", tag=f"x_raw{u}", align_bytes=256) for u in range(2)]
         x_rows = xT.rearrange("(p u h) t -> p u h t", u=2, h=2)
         nc.sync.dma_start(x_raw[0][:], x_rows[:, 0])
         nc.sync.dma_start(offsets[:], offs)
@@ -54,13 +54,13 @@ def tile_moe_shr_glu_gelu_kernel(tc, xT, w1, w3, w2, gate, offs, out):
         wide = {}
 
         def load(name, src, e, before=0, after=0):
-            wide[name, e] = keep.tile([P, before + PACK * H + after], F32, name=f"{name}_raw{e}", align_bytes=64)
+            wide[name, e] = keep.tile([P, before + PACK * H + after], F32, name=f"{name}_raw{e}", align_bytes=256)
             flat = wide[name, e][:, before : before + PACK * H]
             raw[name, e] = flat.rearrange("p (j c) -> p j c", j=PACK)
             nc.sync.dma_start(flat, src[e].rearrange("(p j) c -> p (j c)", j=PACK))
 
         def load_w2(lo, hi):
-            raw["w2", lo] = keep.tile([P, hi - lo, PACK * N], F32, name=f"w2_raw{lo}", align_bytes=64)
+            raw["w2", lo] = keep.tile([P, hi - lo, PACK * N], F32, name=f"w2_raw{lo}", align_bytes=256)
             nc.sync.dma_start(raw["w2", lo][:], w2[lo:hi].rearrange("e (p j) n -> p e (j n)", j=PACK))
 
         identity = keep.tile([P, P], F32, name="identity")
@@ -78,10 +78,10 @@ def tile_moe_shr_glu_gelu_kernel(tc, xT, w1, w3, w2, gate, offs, out):
         load("w3", w3, 1, 0, C)
         load("w1", w1, 0, MARGIN)
         load("w3", w3, 0, 0, C * PACK)
-        ahead = MARGIN - LAP
-        w2_one = keep.tile([P, ahead + PACK * N], F32, name="w2_one", align_bytes=64)
+        ahead = MARGIN
+        w2_one = keep.tile([P, ahead + PACK * N], F32, name="w2_one", align_bytes=256)
         nc.sync.dma_start(w2_one[:, ahead:], w2[1].rearrange("(p j) n -> p (j n)", j=PACK))
-        raw["w2", 0] = tail.tile([P, 1, PACK * N], F32, name="w2_raw0", align_bytes=64, offset=0)
+        raw["w2", 0] = tail.tile([P, 1, PACK * N], F32, name="w2_raw0", align_bytes=256, offset=0)
         nc.sync.dma_start(raw["w2", 0][:], w2[0:1].rearrange("e (p j) n -> p e (j n)", j=PACK))
 
         tiny = keep.tile([P, 2], F32, name="tiny")
@@ -222,7 +222,7 @@ def tile_moe_shr_glu_gelu_kernel(tc, xT, w1, w3, w2, gate, offs, out):
                 stop=True,
             )
 
-        result = keep.tile([P, T], F32, name="result")
+        result = keep.tile([P, T], F32, name="result", align_bytes=256)
         weighted = {}
 
         shared_acc = psum.tile([P, T], F32, name="shared_acc")
@@ -333,7 +333,7 @@ def tile_moe_shr_glu_gelu_kernel(tc, xT, w1, w3, w2, gate, offs, out):
                 scales=scales["w2", 1][:, lo : lo + N // 2],
                 in_=grouped["w2", 1][:, lo * PACK : (lo + N // 2) * PACK],
             )
-        key = new_hidden([(0, 0)], w2_one[:, :MARGIN].bitcast(BF16))
+        key = new_hidden([(0, 0)], w2_one[:, LAP : LAP + MARGIN].bitcast(BF16))
         codes[key] = tail.tile([P, C], U32, name="last_codes", align_bytes=64, offset=0)
         product(0, 0)
         routed_second(1)

@@ -88,11 +88,11 @@ def tile_moe_shr_glu_gelu_kernel(tc, xT, w1, w3, w2, gate, offs, out):
         nc.gpsimd.memset(tiny[:], 0.0)
         nc.scalar.activation(tiny[:, 1:2], tiny[:, 0:1], GELU)
 
-        x_pairs = [keep.tile([P, T, 2], BF16, name=f"x_pairs{u}", align_bytes=64) for u in range(2)]
-        x_slots = keep.tile([P, T, PACK], BF16, name="x_slots", align_bytes=64)
+        x_pairs = [keep.tile([P, T, 2], BF16, name=f"x_pairs{u}", align_bytes=256) for u in range(2)]
+        x_slots = keep.tile([P, T, PACK], BF16, name="x_slots", align_bytes=256)
         x_words = x_slots[:].rearrange("p s j -> p (s j)").bitcast(U32).rearrange("p (s u) -> p s u", u=2)
-        x_codes = keep.tile([P, T], U32, name="x_codes", align_bytes=64)
-        x_scales = keep.tile([P, T], U8, name="x_scales", align_bytes=64)
+        x_codes = keep.tile([P, T], U32, name="x_codes", align_bytes=256)
+        x_scales = keep.tile([P, T], U8, name="x_scales", align_bytes=256)
         nc.vector.tensor_copy(x_pairs[0][:], x_raw[0][:].rearrange("p h t -> p t h"))
         nc.scalar.copy(x_pairs[1][:], x_raw[1][:].rearrange("p h t -> p t h"))
         for u in range(2):
@@ -121,10 +121,10 @@ def tile_moe_shr_glu_gelu_kernel(tc, xT, w1, w3, w2, gate, offs, out):
         def new_operand(key, width, source=None):
             label = "_".join(str(part) for part in key)
             if source is None:
-                source = keep.tile([P, width * PACK], BF16, name=f"grouped_{label}", align_bytes=64)[:]
+                source = keep.tile([P, width * PACK], BF16, name=f"grouped_{label}", align_bytes=256)[:]
             grouped[key] = source
-            codes[key] = keep.tile([P, width], U32, name=f"codes_{label}", align_bytes=64)
-            scales[key] = keep.tile([P, width], U8, name=f"scales_{label}", align_bytes=64)
+            codes[key] = keep.tile([P, width], U32, name=f"codes_{label}", align_bytes=256)
+            scales[key] = keep.tile([P, width], U8, name=f"scales_{label}", align_bytes=256)
 
         def quantize(key, parts=1):
             step = codes[key].shape[1] // parts
@@ -135,14 +135,17 @@ def tile_moe_shr_glu_gelu_kernel(tc, xT, w1, w3, w2, gate, offs, out):
                     in_=grouped[key][:, lo * PACK : (lo + step) * PACK],
                 )
 
-        def cast_first(name, e, front, cut=0):
-            new_operand((name, e), H)
+        def cast_groups(copy, name, e, lo, hi):
             dst = grouped[name, e].rearrange("p (t m a b) -> p m a t b", t=PACK, a=2, b=2)
             src = raw[name, e].rearrange("p (a b) (m t) -> p m a t b", b=2, t=PACK)
+            copy(dst[:, lo:hi], src[:, lo:hi])
+
+        def cast_first(name, e, front, cut=0, later=0):
+            new_operand((name, e), H)
             if cut:
-                nc.vector.tensor_copy(dst[:, :cut], src[:, :cut])
-            nc.vector.tensor_copy(dst[:, cut:front], src[:, cut:front])
-            nc.scalar.copy(dst[:, front:], src[:, front:])
+                cast_groups(nc.vector.tensor_copy, name, e, 0, cut)
+            cast_groups(nc.vector.tensor_copy, name, e, cut, front - later)
+            cast_groups(nc.scalar.copy, name, e, front, P)
 
         def cast_last(name, e, on_vector):
             new_operand((name, e), H)
@@ -278,7 +281,10 @@ def tile_moe_shr_glu_gelu_kernel(tc, xT, w1, w3, w2, gate, offs, out):
         for e in (3, 2, 1, 0):
             units = [(SHARED, 0), (e, e)] if e == 3 else [(e, e)]
             share = V_TWO if len(waiting) >= 2 else V_ONE
-            cast_first("w1", e, share, share // 4 * 2)
+            if len(waiting) > 1:
+                cast_first("w1", e, share, share // 4 * 2)
+            else:
+                cast_first("w1", e, share, 8, share - 24)
             if e == 3:
                 nc.scalar.copy(gates, spread[:].rearrange("p (e s) -> p e s", e=E))
             pair = waiting[:2]
@@ -289,6 +295,8 @@ def tile_moe_shr_glu_gelu_kernel(tc, xT, w1, w3, w2, gate, offs, out):
                 product(*unit)
             if len(waiting) > 1:
                 quantize(("w1", e))
+            else:
+                cast_groups(nc.vector.tensor_copy, "w1", e, 24, share)
             for key in keys:
                 quantize(key)
             if len(waiting) == 1:
@@ -318,7 +326,12 @@ def tile_moe_shr_glu_gelu_kernel(tc, xT, w1, w3, w2, gate, offs, out):
                 gelu(*unit, rows_of(e, V_WIDE if e < 3 else V_W3, i))
             waiting = units
         cast_last("w3", 0, V_LAST)
-        quantize(("w3", 0), 2)
+        for lo, hi in ((0, 2 * P), (2 * P, 3 * P), (3 * P, H)):
+            nc.vector.quantize_mx(
+                out=codes["w3", 0][:, lo:hi].bitcast(FP8X4),
+                scales=scales["w3", 0][:, lo:hi],
+                in_=grouped["w3", 0][:, lo * PACK : hi * PACK],
+            )
         first_layer("w3", 0, 0)
         first = PACK * H - LAP
         gelu(0, 0, wide["w3", 0][:, first : first + C * PACK].rearrange("p (t s) -> p t s", t=PACK))
@@ -334,13 +347,13 @@ def tile_moe_shr_glu_gelu_kernel(tc, xT, w1, w3, w2, gate, offs, out):
                 in_=grouped["w2", 1][:, lo * PACK : (lo + N // 2) * PACK],
             )
         key = new_hidden([(0, 0)], w2_one[:, LAP : LAP + MARGIN].bitcast(BF16))
-        codes[key] = tail.tile([P, C], U32, name="last_codes", align_bytes=64, offset=0)
+        codes[key] = tail.tile([P, C], U32, name="last_codes", align_bytes=256, offset=0)
         product(0, 0)
         routed_second(1)
         cast_second(0)
         quantize(("w2", 0))
         quantize(key)
-        last_shared = tail.tile([P, HALF], F32, name="last_shared", align_bytes=64, offset=C * 4)
+        last_shared = tail.tile([P, HALF], F32, name="last_shared", align_bytes=256, offset=C * 4)
         nc.scalar.copy(last_shared[:], shared_acc[:, :HALF])
         for g in range(2):
             shared_out[g] = last_shared[:, g * C : (g + 1) * C]

@@ -20,16 +20,18 @@ P = 128
 PACK = 4
 SHARED = E
 HALF = T // 2
-
-V_FIRST = 32
-V_HALF = 64
-V_W3 = 48
-V_ONE = 48
-V_WIDE = 80
-V_TWO = 68
-V_LAST = 80
-MARGIN = C * PACK // 2
+LIST_ROWS = 16
+ALIGN = 256
+HIDDEN_WORDS = C * PACK // 2
 LAP = 16
+
+V_SHARED_W1 = 32
+V_SHARED_W3 = 64
+V_BESIDE_TWO = (2 * HIDDEN_WORDS - (HIDDEN_WORDS - LAP)) // PACK
+V_LIGHT = 48
+V_HEAVY = 80
+FIRST_PIECE = 8
+SECOND_PIECE = 24
 
 
 def tile_moe_shr_glu_gelu_kernel(tc, xT, w1, w3, w2, gate, offs, out):
@@ -39,8 +41,8 @@ def tile_moe_shr_glu_gelu_kernel(tc, xT, w1, w3, w2, gate, offs, out):
         tail = ctx.enter_context(tc.tile_pool(name="tail", bufs=1))
         psum = ctx.enter_context(tc.psum_pool(name="psum", bufs=1))
 
-        offsets = keep.tile([P, T // 16], U16, name="offsets")
-        x_raw = [keep.tile([P, 2, T], F32, name=f"x_raw{u}", tag=f"x_raw{u}", align_bytes=256) for u in range(2)]
+        offsets = keep.tile([P, T // LIST_ROWS], U16, name="offsets")
+        x_raw = [keep.tile([P, 2, T], F32, name=f"x_raw{u}", tag=f"x_raw{u}", align_bytes=ALIGN) for u in range(2)]
         x_rows = xT.rearrange("(p u h) t -> p u h t", u=2, h=2)
         nc.sync.dma_start(x_raw[0][:], x_rows[:, 0])
         nc.sync.dma_start(offsets[:], offs)
@@ -49,58 +51,57 @@ def tile_moe_shr_glu_gelu_kernel(tc, xT, w1, w3, w2, gate, offs, out):
         nc.scalar.dma_start(gate_rows[:E], gate[0].rearrange("(e s) -> e s", e=E))
         nc.sync.dma_start(x_raw[1][:], x_rows[:, 1])
 
+        wide = {}
         raw = {}
 
-        wide = {}
-
-        def load(name, src, e, before=0, after=0):
-            wide[name, e] = keep.tile([P, before + PACK * H + after], F32, name=f"{name}_raw{e}", align_bytes=256)
+        def load_first(name, src, e, before=0, after=0):
+            wide[name, e] = keep.tile([P, before + PACK * H + after], F32, name=f"{name}_raw{e}", align_bytes=ALIGN)
             flat = wide[name, e][:, before : before + PACK * H]
             raw[name, e] = flat.rearrange("p (j c) -> p j c", j=PACK)
             nc.sync.dma_start(flat, src[e].rearrange("(p j) c -> p (j c)", j=PACK))
 
-        def load_w2(lo, hi):
-            raw["w2", lo] = keep.tile([P, hi - lo, PACK * N], F32, name=f"w2_raw{lo}", align_bytes=256)
+        def load_second(lo, hi):
+            raw["w2", lo] = keep.tile([P, hi - lo, PACK * N], F32, name=f"w2_raw{lo}", align_bytes=ALIGN)
             nc.sync.dma_start(raw["w2", lo][:], w2[lo:hi].rearrange("e (p j) n -> p e (j n)", j=PACK))
 
         identity = keep.tile([P, P], F32, name="identity")
         make_identity(nc, identity[:])
 
-        load("w1", w1, SHARED)
-        load("w3", w3, SHARED)
-        load("w1", w1, 3, MARGIN)
-        load("w3", w3, 3)
-        load("w1", w1, 2, MARGIN)
-        load_w2(3, 5)
-        load("w3", w3, 2, 0, C)
-        load("w1", w1, 1, MARGIN)
-        load_w2(2, 3)
-        load("w3", w3, 1, 0, C)
-        load("w1", w1, 0, MARGIN)
-        load("w3", w3, 0, 0, C * PACK)
-        ahead = MARGIN
-        w2_one = keep.tile([P, ahead + PACK * N], F32, name="w2_one", align_bytes=256)
-        nc.sync.dma_start(w2_one[:, ahead:], w2[1].rearrange("(p j) n -> p (j n)", j=PACK))
-        raw["w2", 0] = tail.tile([P, 1, PACK * N], F32, name="w2_raw0", align_bytes=256, offset=0)
+        load_first("w1", w1, SHARED)
+        load_first("w3", w3, SHARED)
+        load_first("w1", w1, 3, HIDDEN_WORDS)
+        load_first("w3", w3, 3)
+        load_first("w1", w1, 2, HIDDEN_WORDS)
+        load_second(3, 5)
+        load_first("w3", w3, 2, 0, C)
+        load_first("w1", w1, 1, HIDDEN_WORDS)
+        load_second(2, 3)
+        load_first("w3", w3, 1, 0, C)
+        load_first("w1", w1, 0, HIDDEN_WORDS)
+        load_first("w3", w3, 0, 0, C * PACK)
+        w2_one = keep.tile([P, HIDDEN_WORDS + PACK * N], F32, name="w2_one", align_bytes=ALIGN)
+        nc.sync.dma_start(w2_one[:, HIDDEN_WORDS:], w2[1].rearrange("(p j) n -> p (j n)", j=PACK))
+        raw["w2", 0] = tail.tile([P, 1, PACK * N], F32, name="w2_raw0", align_bytes=ALIGN, offset=0)
         nc.sync.dma_start(raw["w2", 0][:], w2[0:1].rearrange("e (p j) n -> p e (j n)", j=PACK))
 
-        tiny = keep.tile([P, 2], F32, name="tiny")
-        nc.gpsimd.memset(tiny[:], 0.0)
-        nc.scalar.activation(tiny[:, 1:2], tiny[:, 0:1], GELU)
+        table_probe = keep.tile([P, 2], F32, name="table_probe")
+        nc.gpsimd.memset(table_probe[:], 0.0)
+        nc.scalar.activation(table_probe[:, 1:2], table_probe[:, 0:1], GELU)
 
-        x_pairs = [keep.tile([P, T, 2], BF16, name=f"x_pairs{u}", align_bytes=256) for u in range(2)]
-        x_slots = keep.tile([P, T, PACK], BF16, name="x_slots", align_bytes=256)
-        x_words = x_slots[:].rearrange("p s j -> p (s j)").bitcast(U32).rearrange("p (s u) -> p s u", u=2)
-        x_codes = keep.tile([P, T], U32, name="x_codes", align_bytes=256)
-        x_scales = keep.tile([P, T], U8, name="x_scales", align_bytes=256)
+        x_pairs = [keep.tile([P, T, 2], BF16, name=f"x_pairs{u}", align_bytes=ALIGN) for u in range(2)]
+        x_slots = keep.tile([P, T, PACK], BF16, name="x_slots", align_bytes=ALIGN)
+        x_flat = x_slots[:].rearrange("p s j -> p (s j)")
+        x_words = x_flat.bitcast(U32).rearrange("p (s u) -> p s u", u=2)
+        x_codes = keep.tile([P, T], U32, name="x_codes", align_bytes=ALIGN)
+        x_scales = keep.tile([P, T], U8, name="x_scales", align_bytes=ALIGN)
         nc.vector.tensor_copy(x_pairs[0][:], x_raw[0][:].rearrange("p h t -> p t h"))
         nc.scalar.copy(x_pairs[1][:], x_raw[1][:].rearrange("p h t -> p t h"))
         for u in range(2):
             window = x_pairs[u][:].rearrange("p t h -> p (t h)").bitcast(U32)
-            for s in (1, 0):
+            for lo in (HALF, 0):
                 nc.vector.tensor_copy(
-                    x_words[:, s * HALF : (s + 1) * HALF, u],
-                    window.indirect(offsets[:, s * HALF // 16 : (s + 1) * HALF // 16]),
+                    x_words[:, lo : lo + HALF, u],
+                    window.indirect(offsets[:, lo // LIST_ROWS : (lo + HALF) // LIST_ROWS]),
                 )
 
         turned = psum.tile([P, P], F32, name="routed_acc", bufs=2)
@@ -112,60 +113,66 @@ def tile_moe_shr_glu_gelu_kernel(tc, xT, w1, w3, w2, gate, offs, out):
             nc.tensor.transpose(
                 spread[:, e * C : (e + 1) * C], gate_columns[:, e : e + 1].to_broadcast([P, P]), identity[:]
             )
+        gates = raw["w1", 3][:, :, V_BESIDE_TWO * PACK : V_BESIDE_TWO * PACK + C]
 
-        gates = raw["w1", 3][:, :, V_TWO * PACK : V_TWO * PACK + C]
+        grouped = {}
         codes = {}
         scales = {}
-        grouped = {}
 
-        def new_operand(key, width, source=None):
+        def new_operand(key, width, values=None, words=None):
             label = "_".join(str(part) for part in key)
-            if source is None:
-                source = keep.tile([P, width * PACK], BF16, name=f"grouped_{label}", align_bytes=256)[:]
-            grouped[key] = source
-            codes[key] = keep.tile([P, width], U32, name=f"codes_{label}", align_bytes=256)
-            scales[key] = keep.tile([P, width], U8, name=f"scales_{label}", align_bytes=256)
+            if values is None:
+                values = keep.tile([P, width * PACK], BF16, name=f"grouped_{label}", align_bytes=ALIGN)[:]
+            if words is None:
+                words = keep.tile([P, width], U32, name=f"codes_{label}", align_bytes=ALIGN)
+            grouped[key] = values
+            codes[key] = words
+            scales[key] = keep.tile([P, width], U8, name=f"scales_{label}", align_bytes=ALIGN)
 
-        def quantize(key, parts=1):
-            step = codes[key].shape[1] // parts
-            for lo in range(0, parts * step, step):
-                nc.vector.quantize_mx(
-                    out=codes[key][:, lo : lo + step].bitcast(FP8X4),
-                    scales=scales[key][:, lo : lo + step],
-                    in_=grouped[key][:, lo * PACK : (lo + step) * PACK],
-                )
+        def quantize(key, lo=0, hi=None):
+            cols = slice(lo, codes[key].shape[1] if hi is None else hi)
+            nc.vector.quantize_mx(
+                out=codes[key][:, cols].bitcast(FP8X4),
+                scales=scales[key][:, cols],
+                in_=grouped[key][:, cols.start * PACK : cols.stop * PACK],
+            )
 
-        def cast_groups(copy, name, e, lo, hi):
+        def quantize_halves(key):
+            quantize(key, 0, H // 2)
+            quantize(key, H // 2, H)
+
+        def quad_views(name, e):
             dst = grouped[name, e].rearrange("p (t m a b) -> p m a t b", t=PACK, a=2, b=2)
             src = raw[name, e].rearrange("p (a b) (m t) -> p m a t b", b=2, t=PACK)
+            return dst, src
+
+        def cast_quads(copy, name, e, lo, hi):
+            dst, src = quad_views(name, e)
             copy(dst[:, lo:hi], src[:, lo:hi])
 
-        def cast_first(name, e, front, cut=0, later=0):
+        def cast_first(name, e, vector_cuts, scalar_from):
             new_operand((name, e), H)
-            if cut:
-                cast_groups(nc.vector.tensor_copy, name, e, 0, cut)
-            cast_groups(nc.vector.tensor_copy, name, e, cut, front - later)
-            cast_groups(nc.scalar.copy, name, e, front, P)
+            for lo, hi in zip((0, *vector_cuts), vector_cuts):
+                cast_quads(nc.vector.tensor_copy, name, e, lo, hi)
+            cast_quads(nc.scalar.copy, name, e, scalar_from, P)
 
-        def cast_last(name, e, on_vector):
-            new_operand((name, e), H)
-            dst = grouped[name, e].rearrange("p (t m a b) -> p m a t b", t=PACK, a=2, b=2)
-            src = raw[name, e].rearrange("p (a b) (m t) -> p m a t b", b=2, t=PACK)
-            edge = P - LAP // PACK
-            nc.scalar.copy(dst[:, edge:], src[:, edge:])
-            for t in (0, 2):
-                nc.vector.tensor_copy(dst[:, :on_vector, :, t : t + 2], src[:, :on_vector, :, t : t + 2])
-                nc.scalar.copy(dst[:, on_vector:edge, :, t : t + 2], src[:, on_vector:edge, :, t : t + 2])
+        def second_views(values, rows):
+            dst = values.rearrange("p (c i a b) -> p c a i b", i=PACK, a=2, b=2)
+            src = rows.rearrange("p (a b c i) -> p c a i b", i=PACK, a=2, b=2)
+            return dst, src
 
         def cast_second(lo):
-            new_operand(("w2", lo), raw["w2", lo].shape[1] * N)
-            dst = grouped["w2", lo].rearrange("p (e c i a b) -> p e c a i b", i=PACK, a=2, b=2, c=N // PACK)
-            src = raw["w2", lo][:].rearrange("p e (a b c i) -> p e c a i b", i=PACK, a=2, b=2)
-            for e in range(dst.shape[1]):
-                nc.scalar.copy(dst[:, e], src[:, e])
+            count = raw["w2", lo].shape[1]
+            new_operand(("w2", lo), count * N)
+            for i in range(count):
+                values = grouped["w2", lo][:, i * N * PACK : (i + 1) * N * PACK]
+                nc.scalar.copy(*second_views(values, raw["w2", lo][:, i]))
 
         sums = {}
         gelus = {}
+        hidden = {}
+        weighted = {}
+        shared_out = {}
 
         def first_layer(name, e, g):
             acc = psum.tile([P, PACK, C], F32, name=f"{name}_acc", bufs=2 if name == "w1" else 3)
@@ -183,21 +190,29 @@ def tile_moe_shr_glu_gelu_kernel(tc, xT, w1, w3, w2, gate, offs, out):
                     stop=True,
                 )
 
-        shared_out = {}
+        def warm_up(key, cols):
+            idle = psum.tile([P, T], F32, name="w3_acc", bufs=3)
+            nc.tensor.matmul_mx(
+                out=idle[:],
+                lhsT=codes[key][:, cols].bitcast(FP8X4),
+                lhsT_scale=scales[key][:, cols],
+                rhs=x_codes[:].bitcast(FP8X4),
+                rhs_scale=x_scales[:],
+                start=True,
+                stop=True,
+            )
 
-        def rows_of(host, on_vector, i):
-            first = on_vector * PACK + i * C
-            return raw["w3", host][:, :, first : first + C]
+        def scalar_rows(e, scalar_from, i):
+            first = scalar_from * PACK + i * C
+            return raw["w3", e][:, :, first : first + C]
 
         def gelu(e, g, rows):
             gelus[e, g] = rows
             nc.scalar.activation(rows, sums["w1", e, g][:], GELU)
 
-        hidden = {}
-
-        def new_hidden(units, source):
+        def new_hidden(units, values, words=None):
             key = ("h", *units[-1])
-            new_operand(key, len(units) * C, source)
+            new_operand(key, len(units) * C, values, words)
             for i, unit in enumerate(units):
                 hidden[unit] = (key, i)
             return key
@@ -212,7 +227,7 @@ def tile_moe_shr_glu_gelu_kernel(tc, xT, w1, w3, w2, gate, offs, out):
             )
 
         def second_layer(acc, e, g):
-            lo = min(e, 3)
+            lo = min(e, SHARED - 1)
             cols = slice((e - lo) * N, (e - lo + 1) * N)
             key, i = hidden[e, g]
             nc.tensor.matmul_mx(
@@ -225,139 +240,134 @@ def tile_moe_shr_glu_gelu_kernel(tc, xT, w1, w3, w2, gate, offs, out):
                 stop=True,
             )
 
-        result = keep.tile([P, T], F32, name="result", align_bytes=256)
-        weighted = {}
-
+        result = keep.tile([P, T], F32, name="result", align_bytes=ALIGN)
         shared_acc = psum.tile([P, T], F32, name="shared_acc")
 
-        def shared_second(g):
-            second_layer(shared_acc[:, g * C : (g + 1) * C], SHARED, g)
-
-        def shared_leave(lo, hi, host):
-            first = PACK * H - LAP
-            nc.scalar.copy(wide["w3", host][:, first : first + (hi - lo) * C], shared_acc[:, lo * C : hi * C])
-            for g in range(lo, hi):
-                shared_out[g] = wide["w3", host][:, first + (g - lo) * C : first + (g - lo + 1) * C]
-
-        def routed_second(e, host=None):
+        def routed_second(e, place):
             acc = psum.tile([P, C], F32, name="routed_acc", bufs=2)
             second_layer(acc[:], e, e)
-            if host is None:
-                weighted[e] = keep.tile([P, C], F32, name=f"weighted{e}")[:]
-            else:
-                weighted[e] = wide["w3", host][:, :C]
-            nc.vector.tensor_tensor(weighted[e], acc[:], gates[:, e], MULT)
+            weighted[e] = place
+            nc.vector.tensor_tensor(place, acc[:], gates[:, e], MULT)
 
         def scatter(e):
             nc.vector.tensor_tensor(
-                result[:].indirect(offsets[:, e * C // 16 : (e + 1) * C // 16]),
+                result[:].indirect(offsets[:, e * C // LIST_ROWS : (e + 1) * C // LIST_ROWS]),
                 weighted[e],
                 shared_out[e],
                 ADD,
             )
 
-        x_flat = x_slots[:].rearrange("p s j -> p (s j)")
+        after_rows = PACK * H - LAP
+
         for lo in (HALF, 0):
             nc.vector.quantize_mx(
                 out=x_codes[:, lo : lo + HALF].bitcast(FP8X4),
                 scales=x_scales[:, lo : lo + HALF],
                 in_=x_flat[:, lo * PACK : (lo + HALF) * PACK],
             )
-        cast_first("w1", SHARED, V_FIRST)
+        cast_first("w1", SHARED, [V_SHARED_W1], V_SHARED_W1)
         quantize(("w1", SHARED))
-        cast_first("w3", SHARED, V_HALF)
+        cast_first("w3", SHARED, [V_SHARED_W3], V_SHARED_W3)
         waiting = [(SHARED, 3), (SHARED, 2), (SHARED, 1)]
         for unit in waiting[:2]:
             first_layer("w1", *unit)
-        quantize(("w3", SHARED), 2)
+        quantize_halves(("w3", SHARED))
         for unit in waiting:
             first_layer("w3", *unit)
         for i, unit in enumerate(waiting[:2]):
-            gelu(*unit, rows_of(SHARED, V_HALF, i))
+            gelu(*unit, scalar_rows(SHARED, V_SHARED_W3, i))
         first_layer("w1", *waiting[2])
-        third = keep.tile([P, PACK, C], F32, name="third")
-        gelu(*waiting[2], third[:])
+        third_gelu = keep.tile([P, PACK, C], F32, name="third_gelu")
+        gelu(*waiting[2], third_gelu[:])
 
-        for e in (3, 2, 1, 0):
-            units = [(SHARED, 0), (e, e)] if e == 3 else [(e, e)]
-            share = V_TWO if len(waiting) >= 2 else V_ONE
-            if len(waiting) > 1:
-                cast_first("w1", e, share, share // 4 * 2)
+        for e in range(E - 1, -1, -1):
+            first_round = e == E - 1
+            units = [(SHARED, 0), (e, e)] if first_round else [(e, e)]
+            several = len(waiting) > 1
+            if several:
+                cast_first("w1", e, [V_BESIDE_TWO // 2, V_BESIDE_TWO], V_BESIDE_TWO)
             else:
-                cast_first("w1", e, share, 8, share - 24)
-            if e == 3:
+                cast_first("w1", e, [FIRST_PIECE, SECOND_PIECE], V_LIGHT)
+            if first_round:
                 nc.scalar.copy(gates, spread[:].rearrange("p (e s) -> p e s", e=E))
             pair = waiting[:2]
-            keys = [new_hidden(pair, wide["w1", e][:, LAP : LAP + len(pair) * MARGIN].bitcast(BF16))]
-            if len(waiting) == 3:
-                keys.append(new_hidden(waiting[2:], raw["w1", e][:, 1, :MARGIN].bitcast(BF16)))
+            keys = [new_hidden(pair, wide["w1", e][:, LAP : LAP + len(pair) * HIDDEN_WORDS].bitcast(BF16))]
+            if first_round:
+                keys.append(new_hidden(waiting[2:], raw["w1", e][:, 1, :HIDDEN_WORDS].bitcast(BF16)))
             for unit in waiting:
                 product(*unit)
-            if len(waiting) > 1:
+            if several:
                 quantize(("w1", e))
             else:
-                cast_groups(nc.vector.tensor_copy, "w1", e, 24, share)
+                cast_quads(nc.vector.tensor_copy, "w1", e, SECOND_PIECE, V_LIGHT)
             for key in keys:
                 quantize(key)
-            if len(waiting) == 1:
+            if e == 0:
+                warm_up(keys[0], slice(0, P))
+            if not several:
                 quantize(("w1", e))
-            if e == 3:
+            if first_round:
                 first_layer("w3", SHARED, 0)
             for unit in units:
                 first_layer("w1", *unit)
             if e == 0:
+                warm_up(("w1", 0), slice(3 * P, H))
                 break
-            if e < 3:
+            if first_round:
+                on_vector = V_LIGHT
+                cast_first("w3", e, [on_vector], on_vector)
+                quantize_halves(("w3", e))
+                first_layer("w3", e, e)
+            else:
+                on_vector = V_HEAVY
                 cast_second(e + 1)
                 quantize(("w2", e + 1))
-            cast_first("w3", e, V_WIDE if e < 3 else V_W3, C // PACK if e < 3 else 0)
-            if e < 3:
-                routed_second(e + 1, e)
-            quantize(("w3", e), 2 if e == 3 else 1)
-            first_layer("w3", e, e)
-            if e == 2:
-                for g in (3, 2, 1, 0):
-                    shared_second(g)
-            if e < 3:
-                shared_leave(e + 1, e + 2, e)
-            if e < 3:
+                cast_first("w3", e, [C // PACK, on_vector], on_vector)
+                routed_second(e + 1, wide["w3", e][:, :C])
+                quantize(("w3", e))
+                first_layer("w3", e, e)
+                if e == 1:
+                    warm_up(("w3", 1), slice(3 * P, H))
+                if e == E - 2:
+                    for g in range(E - 1, -1, -1):
+                        second_layer(shared_acc[:, g * C : (g + 1) * C], SHARED, g)
+                shared_out[e + 1] = wide["w3", e][:, after_rows : after_rows + C]
+                nc.scalar.copy(shared_out[e + 1], shared_acc[:, (e + 1) * C : (e + 2) * C])
                 scatter(e + 1)
             for i, unit in enumerate(units):
-                gelu(*unit, rows_of(e, V_WIDE if e < 3 else V_W3, i))
+                gelu(*unit, scalar_rows(e, on_vector, i))
             waiting = units
-        cast_last("w3", 0, V_LAST)
+
+        new_operand(("w3", 0), H)
+        dst, src = quad_views("w3", 0)
+        edge = P - LAP // PACK
+        nc.scalar.copy(dst[:, edge:], src[:, edge:])
+        for t in (0, 2):
+            nc.vector.tensor_copy(dst[:, :V_HEAVY, :, t : t + 2], src[:, :V_HEAVY, :, t : t + 2])
+            nc.scalar.copy(dst[:, V_HEAVY:edge, :, t : t + 2], src[:, V_HEAVY:edge, :, t : t + 2])
         for lo, hi in ((0, 2 * P), (2 * P, 3 * P), (3 * P, H)):
-            nc.vector.quantize_mx(
-                out=codes["w3", 0][:, lo:hi].bitcast(FP8X4),
-                scales=scales["w3", 0][:, lo:hi],
-                in_=grouped["w3", 0][:, lo * PACK : hi * PACK],
-            )
+            quantize(("w3", 0), lo, hi)
         first_layer("w3", 0, 0)
-        first = PACK * H - LAP
-        gelu(0, 0, wide["w3", 0][:, first : first + C * PACK].rearrange("p (t s) -> p t s", t=PACK))
+        warm_up(("w3", 0), slice(3 * P, H))
+        gelu(0, 0, wide["w3", 0][:, after_rows : after_rows + C * PACK].rearrange("p (t s) -> p t s", t=PACK))
         new_operand(("w2", 1), N, grouped["w3", 0][:, : N * PACK])
-        dst = grouped["w2", 1].rearrange("p (c i a b) -> p c a i b", i=PACK, a=2, b=2)
-        src = w2_one[:, ahead:].rearrange("p (a b c i) -> p c a i b", i=PACK, a=2, b=2)
-        for half in (slice(N // 8, N // 4), slice(0, N // 8)):
-            nc.vector.tensor_copy(dst[:, half], src[:, half])
+        dst, src = second_views(grouped["w2", 1], w2_one[:, HIDDEN_WORDS:])
         for lo in (N // 2, 0):
-            nc.vector.quantize_mx(
-                out=codes["w2", 1][:, lo : lo + N // 2].bitcast(FP8X4),
-                scales=scales["w2", 1][:, lo : lo + N // 2],
-                in_=grouped["w2", 1][:, lo * PACK : (lo + N // 2) * PACK],
-            )
-        key = new_hidden([(0, 0)], w2_one[:, LAP : LAP + MARGIN].bitcast(BF16))
-        codes[key] = tail.tile([P, C], U32, name="last_codes", align_bytes=256, offset=0)
+            nc.vector.tensor_copy(dst[:, lo // PACK : (lo + N // 2) // PACK], src[:, lo // PACK : (lo + N // 2) // PACK])
+        for lo in (N // 2, 0):
+            quantize(("w2", 1), lo, lo + N // 2)
+        last_codes = tail.tile([P, C], U32, name="last_codes", align_bytes=ALIGN, offset=0)
+        last_hidden = new_hidden([(0, 0)], w2_one[:, LAP : LAP + HIDDEN_WORDS].bitcast(BF16), last_codes)
         product(0, 0)
-        routed_second(1)
+        routed_second(1, keep.tile([P, C], F32, name="weighted1")[:])
         cast_second(0)
         quantize(("w2", 0))
-        quantize(key)
-        last_shared = tail.tile([P, HALF], F32, name="last_shared", align_bytes=256, offset=C * 4)
+        quantize(last_hidden)
+        last_shared = tail.tile([P, HALF], F32, name="last_shared", align_bytes=ALIGN, offset=C * 4)
         nc.scalar.copy(last_shared[:], shared_acc[:, :HALF])
         for g in range(2):
             shared_out[g] = last_shared[:, g * C : (g + 1) * C]
         scatter(1)
-        routed_second(0)
+        routed_second(0, keep.tile([P, C], F32, name="weighted0")[:])
         scatter(0)
         nc.sync.dma_start(out, result[:])

@@ -190,18 +190,6 @@ def tile_moe_shr_glu_gelu_kernel(tc, xT, w1, w3, w2, gate, offs, out):
                     stop=True,
                 )
 
-        def warm_up(key, cols):
-            idle = psum.tile([P, T], F32, name="w3_acc", bufs=3)
-            nc.tensor.matmul_mx(
-                out=idle[:],
-                lhsT=codes[key][:, cols].bitcast(FP8X4),
-                lhsT_scale=scales[key][:, cols],
-                rhs=x_codes[:].bitcast(FP8X4),
-                rhs_scale=x_scales[:],
-                start=True,
-                stop=True,
-            )
-
         def scalar_rows(e, scalar_from, i):
             first = scalar_from * PACK + i * C
             return raw["w3", e][:, :, first : first + C]
@@ -302,8 +290,6 @@ def tile_moe_shr_glu_gelu_kernel(tc, xT, w1, w3, w2, gate, offs, out):
                 cast_quads(nc.vector.tensor_copy, "w1", e, SECOND_PIECE, V_LIGHT)
             for key in keys:
                 quantize(key)
-            if e == 0:
-                warm_up(keys[0], slice(0, P))
             if not several:
                 quantize(("w1", e))
             if first_round:
@@ -311,7 +297,6 @@ def tile_moe_shr_glu_gelu_kernel(tc, xT, w1, w3, w2, gate, offs, out):
             for unit in units:
                 first_layer("w1", *unit)
             if e == 0:
-                warm_up(("w1", 0), slice(3 * P, H))
                 break
             if first_round:
                 on_vector = V_LIGHT
@@ -326,8 +311,6 @@ def tile_moe_shr_glu_gelu_kernel(tc, xT, w1, w3, w2, gate, offs, out):
                 routed_second(e + 1, wide["w3", e][:, :C])
                 quantize(("w3", e))
                 first_layer("w3", e, e)
-                if e == 1:
-                    warm_up(("w3", 1), slice(3 * P, H))
                 if e == E - 2:
                     for g in range(E - 1, -1, -1):
                         second_layer(shared_acc[:, g * C : (g + 1) * C], SHARED, g)
@@ -348,7 +331,6 @@ def tile_moe_shr_glu_gelu_kernel(tc, xT, w1, w3, w2, gate, offs, out):
         for lo, hi in ((0, 2 * P), (2 * P, 3 * P), (3 * P, H)):
             quantize(("w3", 0), lo, hi)
         first_layer("w3", 0, 0)
-        warm_up(("w3", 0), slice(3 * P, H))
         gelu(0, 0, wide["w3", 0][:, after_rows : after_rows + C * PACK].rearrange("p (t s) -> p t s", t=PACK))
         new_operand(("w2", 1), N, grouped["w3", 0][:, : N * PACK])
         dst, src = second_views(grouped["w2", 1], w2_one[:, HIDDEN_WORDS:])

from contextlib import ExitStack

import concourse.mybir as mybir
from concourse.masks import make_identity

K, T, E, C, H, N = 512, 512, 4, 128, 512, 128
FLOPS = 2 * (2 * T) * (2 * K * H + H * N)

F32 = mybir.dt.float32
BF16 = mybir.dt.bfloat16
U32 = mybir.dt.uint32
U16 = mybir.dt.uint16
U8 = mybir.dt.uint8
FP8X4 = mybir.dt.float8_e4m3fn_x4
GELU = mybir.ActivationFunctionType.Gelu_apprx_tanh
MULT = mybir.AluOpType.mult
ADD = mybir.AluOpType.add

P = 128
PACK = 4
SHARED = E
HALF = T // 2
LIST_ROWS = 16
ALIGN = 256
HIDDEN_WORDS = C * PACK // 2
LAP = 16

V_SHARED_W1 = 32
V_SHARED_W3 = 64
V_BESIDE_TWO = (2 * HIDDEN_WORDS - (HIDDEN_WORDS - LAP)) // PACK
V_LIGHT = 48
V_HEAVY = 80
FIRST_PIECE = 8
SECOND_PIECE = 24


def tile_moe_shr_glu_gelu_kernel(tc, xT, w1, w3, w2, gate, offs, out):
    nc = tc.nc
    with ExitStack() as ctx:
        keep = ctx.enter_context(tc.tile_pool(name="keep", bufs=1))
        tail = ctx.enter_context(tc.tile_pool(name="tail", bufs=1))
        psum = ctx.enter_context(tc.psum_pool(name="psum", bufs=1))

        offsets = keep.tile([P, T // LIST_ROWS], U16, name="offsets")
        x_raw = [keep.tile([P, 2, T], F32, name=f"x_raw{u}", tag=f"x_raw{u}", align_bytes=ALIGN) for u in range(2)]
        x_rows = xT.rearrange("(p u h) t -> p u h t", u=2, h=2)
        nc.sync.dma_start(x_raw[0][:], x_rows[:, 0])
        nc.sync.dma_start(offsets[:], offs)
        gate_rows = keep.tile([P, C], F32, name="gate_rows")
        nc.vector.memset(gate_rows[:], 0.0)
        nc.scalar.dma_start(gate_rows[:E], gate[0].rearrange("(e s) -> e s", e=E))
        nc.sync.dma_start(x_raw[1][:], x_rows[:, 1])

        wide = {}
        raw = {}

        def load_first(name, src, e, before=0, after=0):
            wide[name, e] = keep.tile([P, before + PACK * H + after], F32, name=f"{name}_raw{e}", align_bytes=ALIGN)
            flat = wide[name, e][:, before : before + PACK * H]
            raw[name, e] = flat.rearrange("p (j c) -> p j c", j=PACK)
            nc.sync.dma_start(flat, src[e].rearrange("(p j) c -> p (j c)", j=PACK))

        def load_second(lo, hi):
            raw["w2", lo] = keep.tile([P, hi - lo, PACK * N], F32, name=f"w2_raw{lo}", align_bytes=ALIGN)
            nc.sync.dma_start(raw["w2", lo][:], w2[lo:hi].rearrange("e (p j) n -> p e (j n)", j=PACK))

        identity = keep.tile([P, P], F32, name="identity")
        make_identity(nc, identity[:])

        load_first("w1", w1, SHARED)
        load_first("w3", w3, SHARED)
        load_first("w1", w1, 3, HIDDEN_WORDS)
        load_first("w3", w3, 3)
        load_first("w1", w1, 2, HIDDEN_WORDS)
        load_second(3, 5)
        load_first("w3", w3, 2, 0, C)
        load_first("w1", w1, 1, HIDDEN_WORDS)
        load_second(2, 3)
        load_first("w3", w3, 1, 0, C)
        load_first("w1", w1, 0, HIDDEN_WORDS)
        load_first("w3", w3, 0, 0, C * PACK)
        w2_one = keep.tile([P, HIDDEN_WORDS + PACK * N], F32, name="w2_one", align_bytes=ALIGN)
        nc.sync.dma_start(w2_one[:, HIDDEN_WORDS:], w2[1].rearrange("(p j) n -> p (j n)", j=PACK))
        raw["w2", 0] = tail.tile([P, 1, PACK * N], F32, name="w2_raw0", align_bytes=ALIGN, offset=0)
        nc.sync.dma_start(raw["w2", 0][:], w2[0:1].rearrange("e (p j) n -> p e (j n)", j=PACK))

        table_probe = keep.tile([P, 2], F32, name="table_probe")
        nc.gpsimd.memset(table_probe[:], 0.0)
        nc.scalar.activation(table_probe[:, 1:2], table_probe[:, 0:1], GELU)

        x_pairs = [keep.tile([P, T, 2], BF16, name=f"x_pairs{u}", align_bytes=ALIGN) for u in range(2)]
        x_slots = keep.tile([P, T, PACK], BF16, name="x_slots", align_bytes=ALIGN)
        x_flat = x_slots[:].rearrange("p s j -> p (s j)")
        x_words = x_flat.bitcast(U32).rearrange("p (s u) -> p s u", u=2)
        x_codes = keep.tile([P, T], U32, name="x_codes", align_bytes=ALIGN)
        x_scales = keep.tile([P, T], U8, name="x_scales", align_bytes=ALIGN)
        nc.vector.tensor_copy(x_pairs[0][:], x_raw[0][:].rearrange("p h t -> p t h"))
        nc.scalar.copy(x_pairs[1][:], x_raw[1][:].rearrange("p h t -> p t h"))
        for u in range(2):
            window = x_pairs[u][:].rearrange("p t h -> p (t h)").bitcast(U32)
            for lo in (HALF, 0):
                nc.vector.tensor_copy(
                    x_words[:, lo : lo + HALF, u],
                    window.indirect(offsets[:, lo // LIST_ROWS : (lo + HALF) // LIST_ROWS]),
                )

        turned = psum.tile([P, P], F32, name="routed_acc", bufs=2)
        nc.tensor.transpose(turned[:], gate_rows[:], identity[:])
        gate_columns = keep.tile([P, E], F32, name="gate_columns")
        nc.scalar.copy(gate_columns[:], turned[:, :E])
        spread = psum.tile([P, T], F32, name="routed_acc", bufs=2)
        for e in range(E):
            nc.tensor.transpose(
                spread[:, e * C : (e + 1) * C], gate_columns[:, e : e + 1].to_broadcast([P, P]), identity[:]
            )
        gates = raw["w1", 3][:, :, V_BESIDE_TWO * PACK : V_BESIDE_TWO * PACK + C]

        grouped = {}
        codes = {}
        scales = {}

        def new_operand(key, width, values=None, words=None):
            label = "_".join(str(part) for part in key)
            if values is None:
                values = keep.tile([P, width * PACK], BF16, name=f"grouped_{label}", align_bytes=ALIGN)[:]
            if words is None:
                words = keep.tile([P, width], U32, name=f"codes_{label}", align_bytes=ALIGN)
            grouped[key] = values
            codes[key] = words
            scales[key] = keep.tile([P, width], U8, name=f"scales_{label}", align_bytes=ALIGN)

        def quantize(key, lo=0, hi=None):
            cols = slice(lo, codes[key].shape[1] if hi is None else hi)
            nc.vector.quantize_mx(
                out=codes[key][:, cols].bitcast(FP8X4),
                scales=scales[key][:, cols],
                in_=grouped[key][:, cols.start * PACK : cols.stop * PACK],
            )

        def quantize_halves(key):
            quantize(key, 0, H // 2)
            quantize(key, H // 2, H)

        def quad_views(name, e):
            dst = grouped[name, e].rearrange("p (t m a b) -> p m a t b", t=PACK, a=2, b=2)
            src = raw[name, e].rearrange("p (a b) (m t) -> p m a t b", b=2, t=PACK)
            return dst, src

        def cast_quads(copy, name, e, lo, hi):
            dst, src = quad_views(name, e)
            copy(dst[:, lo:hi], src[:, lo:hi])

        def cast_first(name, e, vector_cuts, scalar_from):
            new_operand((name, e), H)
            for lo, hi in zip((0, *vector_cuts), vector_cuts):
                cast_quads(nc.vector.tensor_copy, name, e, lo, hi)
            cast_quads(nc.scalar.copy, name, e, scalar_from, P)

        def second_views(values, rows):
            dst = values.rearrange("p (c i a b) -> p c a i b", i=PACK, a=2, b=2)
            src = rows.rearrange("p (a b c i) -> p c a i b", i=PACK, a=2, b=2)
            return dst, src

        def cast_second(lo):
            count = raw["w2", lo].shape[1]
            new_operand(("w2", lo), count * N)
            for i in range(count):
                values = grouped["w2", lo][:, i * N * PACK : (i + 1) * N * PACK]
                nc.scalar.copy(*second_views(values, raw["w2", lo][:, i]))

        sums = {}
        gelus = {}
        hidden = {}
        weighted = {}
        shared_out = {}

        def first_layer(name, e, g):
            acc = psum.tile([P, PACK, C], F32, name=f"{name}_acc", bufs=2 if name == "w1" else 3)
            sums[name, e, g] = acc
            slots = slice(g * C, (g + 1) * C)
            for t in range(PACK):
                cols = slice(t * P, (t + 1) * P)
                nc.tensor.matmul_mx(
                    out=acc[:, t, :],
                    lhsT=codes[name, e][:, cols].bitcast(FP8X4),
                    lhsT_scale=scales[name, e][:, cols],
                    rhs=x_codes[:, slots].bitcast(FP8X4),
                    rhs_scale=x_scales[:, slots],
                    start=True,
                    stop=True,
                )

        def scalar_rows(e, scalar_from, i):
            first = scalar_from * PACK + i * C
            return raw["w3", e][:, :, first : first + C]

        def gelu(e, g, rows):
            gelus[e, g] = rows
            nc.scalar.activation(rows, sums["w1", e, g][:], GELU)

        def new_hidden(units, values, words=None):
            key = ("h", *units[-1])
            new_operand(key, len(units) * C, values, words)
            for i, unit in enumerate(units):
                hidden[unit] = (key, i)
            return key

        def product(e, g):
            key, i = hidden[e, g]
            nc.vector.tensor_tensor(
                grouped[key][:, i * C * PACK : (i + 1) * C * PACK].rearrange("p (q s t) -> p q t s", s=2, t=PACK),
                gelus[e, g].rearrange("p t (q s) -> p q t s", s=2),
                sums["w3", e, g][:].rearrange("p t (q s) -> p q t s", s=2),
                MULT,
            )

        def second_layer(acc, e, g):
            lo = min(e, SHARED - 1)
            cols = slice((e - lo) * N, (e - lo + 1) * N)
            key, i = hidden[e, g]
            nc.tensor.matmul_mx(
                out=acc,
                lhsT=codes["w2", lo][:, cols].bitcast(FP8X4),
                lhsT_scale=scales["w2", lo][:, cols],
                rhs=codes[key][:, i * C : (i + 1) * C].bitcast(FP8X4),
                rhs_scale=scales[key][:, i * C : (i + 1) * C],
                start=True,
                stop=True,
            )

        result = keep.tile([P, T], F32, name="result", align_bytes=ALIGN)
        shared_acc = psum.tile([P, T], F32, name="shared_acc")

        def routed_second(e, place):
            acc = psum.tile([P, C], F32, name="routed_acc", bufs=2)
            second_layer(acc[:], e, e)
            weighted[e] = place
            nc.vector.tensor_tensor(place, acc[:], gates[:, e], MULT)

        def scatter(e):
            nc.vector.tensor_tensor(
                result[:].indirect(offsets[:, e * C // LIST_ROWS : (e + 1) * C // LIST_ROWS]),
                weighted[e],
                shared_out[e],
                ADD,
            )

        after_rows = PACK * H - LAP

        for lo in (HALF, 0):
            nc.vector.quantize_mx(
                out=x_codes[:, lo : lo + HALF].bitcast(FP8X4),
                scales=x_scales[:, lo : lo + HALF],
                in_=x_flat[:, lo * PACK : (lo + HALF) * PACK],
            )
        cast_first("w1", SHARED, [V_SHARED_W1], V_SHARED_W1)
        quantize(("w1", SHARED))
        cast_first("w3", SHARED, [V_SHARED_W3], V_SHARED_W3)
        waiting = [(SHARED, 3), (SHARED, 2), (SHARED, 1)]
        for unit in waiting[:2]:
            first_layer("w1", *unit)
        quantize_halves(("w3", SHARED))
        for unit in waiting:
            first_layer("w3", *unit)
        for i, unit in enumerate(waiting[:2]):
            gelu(*unit, scalar_rows(SHARED, V_SHARED_W3, i))
        first_layer("w1", *waiting[2])
        third_gelu = keep.tile([P, PACK, C], F32, name="third_gelu")
        gelu(*waiting[2], third_gelu[:])

        for e in range(E - 1, -1, -1):
            first_round = e == E - 1
            units = [(SHARED, 0), (e, e)] if first_round else [(e, e)]
            several = len(waiting) > 1
            if several:
                cast_first("w1", e, [V_BESIDE_TWO // 2, V_BESIDE_TWO], V_BESIDE_TWO)
            else:
                cast_first("w1", e, [FIRST_PIECE, SECOND_PIECE], V_LIGHT)
            if first_round:
                nc.scalar.copy(gates, spread[:].rearrange("p (e s) -> p e s", e=E))
            pair = waiting[:2]
            keys = [new_hidden(pair, wide["w1", e][:, LAP : LAP + len(pair) * HIDDEN_WORDS].bitcast(BF16))]
            if first_round:
                keys.append(new_hidden(waiting[2:], raw["w1", e][:, 1, :HIDDEN_WORDS].bitcast(BF16)))
            for unit in waiting:
                product(*unit)
            if several:
                quantize(("w1", e))
            else:
                cast_quads(nc.vector.tensor_copy, "w1", e, SECOND_PIECE, V_LIGHT)
            for key in keys:
                quantize(key)
            if not several:
                quantize(("w1", e))
            if first_round:
                first_layer("w3", SHARED, 0)
            for unit in units:
                first_layer("w1", *unit)
            if e == 0:
                break
            if first_round:
                on_vector = V_LIGHT
                cast_first("w3", e, [on_vector], on_vector)
                quantize_halves(("w3", e))
                first_layer("w3", e, e)
            else:
                on_vector = V_HEAVY
                cast_second(e + 1)
                quantize(("w2", e + 1))
                cast_first("w3", e, [C // PACK, on_vector], on_vector)
                routed_second(e + 1, wide["w3", e][:, :C])
                quantize(("w3", e))
                first_layer("w3", e, e)
                if e == E - 2:
                    for g in range(E - 1, -1, -1):
                        second_layer(shared_acc[:, g * C : (g + 1) * C], SHARED, g)
                shared_out[e + 1] = wide["w3", e][:, after_rows : after_rows + C]
                nc.scalar.copy(shared_out[e + 1], shared_acc[:, (e + 1) * C : (e + 2) * C])
                scatter(e + 1)
            for i, unit in enumerate(units):
                gelu(*unit, scalar_rows(e, on_vector, i))
            waiting = units

        new_operand(("w3", 0), H)
        dst, src = quad_views("w3", 0)
        edge = P - LAP // PACK
        nc.scalar.copy(dst[:, edge:], src[:, edge:])
        for t in (0, 2):
            nc.vector.tensor_copy(dst[:, :V_HEAVY, :, t : t + 2], src[:, :V_HEAVY, :, t : t + 2])
            nc.scalar.copy(dst[:, V_HEAVY:edge, :, t : t + 2], src[:, V_HEAVY:edge, :, t : t + 2])
        for lo, hi in ((0, 2 * P), (2 * P, 3 * P), (3 * P, H)):
            quantize(("w3", 0), lo, hi)
        first_layer("w3", 0, 0)
        gelu(0, 0, wide["w3", 0][:, after_rows : after_rows + C * PACK].rearrange("p (t s) -> p t s", t=PACK))
        new_operand(("w2", 1), N, grouped["w3", 0][:, : N * PACK])
        dst, src = second_views(grouped["w2", 1], w2_one[:, HIDDEN_WORDS:])
        for lo in (N // 2, 0):
            nc.vector.tensor_copy(dst[:, lo // PACK : (lo + N // 2) // PACK], src[:, lo // PACK : (lo + N // 2) // PACK])
        for lo in (N // 2, 0):
            quantize(("w2", 1), lo, lo + N // 2)
        last_codes = tail.tile([P, C], U32, name="last_codes", align_bytes=ALIGN, offset=0)
        last_hidden = new_hidden([(0, 0)], w2_one[:, LAP : LAP + HIDDEN_WORDS].bitcast(BF16), last_codes)
        product(0, 0)
        routed_second(1, keep.tile([P, C], F32, name="weighted1")[:])
        cast_second(0)
        quantize(("w2", 0))
        quantize(last_hidden)
        last_shared = tail.tile([P, HALF], F32, name="last_shared", align_bytes=ALIGN, offset=C * 4)
        nc.scalar.copy(last_shared[:], shared_acc[:, :HALF])
        for g in range(2):
            shared_out[g] = last_shared[:, g * C : (g + 1) * C]
        scatter(1)
        routed_second(0, keep.tile([P, C], F32, name="weighted0")[:])
        scatter(0)
        nc.sync.dma_start(out, result[:])
